import numpy as np, ml_dtypes
CORES = [3,11,19,27,35,43]
N = 6
BF = ml_dtypes.bfloat16
def gentries(a):
    return np.ascontiguousarray(a.reshape(8, 16, -1).transpose(0, 2, 1)).reshape(8, -1)
def gtable(e):
    e = np.asarray(e); return np.ascontiguousarray(e.reshape(8, -1, 16).transpose(0, 2, 1)).reshape(128, -1).astype(np.int32)
F, S, T, LV, C, W = 1984, 256, 4, 2, 6, 3520
LN, SH = (1, 2), (0, 1)
def parts(rng):
    th = rng.integers(0, 4096, (N, 8, 16, F)); su = rng.integers(0, F, (N, 8, 16, F)); st = rng.integers(0, F, (N, 8, LV, S))
    h = F // 8; hot = np.argsort(rng.random((N, 8, F)), axis=-1)[..., :h]
    a = np.take_along_axis(hot, rng.integers(0, h, (N, 8, 16 * F)), 2).reshape(su.shape); su = np.where(rng.random(su.shape) < 0.5, a, su)
    a = np.take_along_axis(hot, rng.integers(0, h, (N, 8, LV * S)), 2).reshape(st.shape); st = np.where(rng.random(st.shape) < 0.75, a, st)
    near = np.take_along_axis(th, rng.integers(0, F, (N, 8, 1, S)), 3)[:, :, :, None, :] + rng.integers(-600, 601, (N, 8, 16, T, S))
    xs = np.where(rng.random((N, 8, 1, 1, S)) < 0.5, np.clip(near, 0, 4095), rng.integers(0, 4096, (N, 8, 16, T, S)))
    hv = (1 + rng.random((N, 8, 16, 16))) * np.exp2(rng.integers(-1, 1, (N, 8, 16, 16)))
    return th, su, st, xs, hv
def pack(th, su, st, xs, hv):
    return {"th": np.ascontiguousarray(th.reshape(N, 128, F)).astype(np.int32), "su": np.ascontiguousarray(su.reshape(N, 128, F)).astype(np.int32),
            "st": np.stack([gtable(a.reshape(8, -1)) for a in st]), "xs": np.ascontiguousarray(xs.reshape(N, 128, T * S)).astype(np.int32),
            "hv": np.ascontiguousarray(hv.reshape(N, 128, 16)).astype(np.float32).astype(BF)}
def setup_inputs(rng):
    return pack(*parts(rng))
def setup_inputs_corners(rng):
    th, su, st, xs, hv = parts(rng); v = np.arange(F)[None, :]; i = np.arange(16)[:, None]
    for q in range(N):
        for g in range(8):
            k = (g + q) % 4; o = su[q, g].copy()
            if k == 0: su[q, g] = np.where(rng.random((1, F)) < 0.5, v, o)
            if k == 1: su[q, g] = (v + i) % F
            if k == 2: su[q, g] = np.where(o % 3 == 0, 0, np.where(o % 3 == 1, F - 1, v))
            if k == 3: su[q, g] = np.where(i == rng.integers(0, 16, (1, F)), o, o[3:4])
    e = rng.random(st.shape); st = np.where(e < 0.15, 0, np.where(e < 0.3, F - 1, st)); st[..., S - 1] = F - 1; st[..., 0] = 0
    return pack(th, su, st, xs, hv)
def setup_inputs_crowd(rng):
    th, su, st, xs, hv = parts(rng)
    for q in range(N):
        for g in range(8):
            k = (g + q) % 4; n = S if k == 3 else 3; x0 = xs[q, g].copy()
            o = rng.permutation(F)[:LV * n].reshape(LV, n); y = rng.integers(0, 4096, (16, n))
            for l in range(LV):
                th[q, g][:, o[l]] = np.clip(y + rng.integers(-60, 61, (16, n)), 0, 4095)
                su[q, g][C::2, o[l]] = o[l]
                su[q, g][C + 1::2, o[l]] = o[l][rng.integers(0, n, (len(range(C + 1, 16, 2)), n))]
            lane = np.arange(S) if k == 3 else rng.integers(0, 3, S) if k == 2 else np.ones(S, np.int64)
            st[q, g] = o[:, lane]; xs[q, g] = np.clip(y[:, None, lane] + rng.integers(-100, 101, (16, T, S)), 0, 4095)
            if k == 1:
                z = 0 if (g >> 2) % 2 == q % 2 else S - 1
                st[q, g, :, z] = (o[:, 1] + 1 + rng.integers(0, F - 1, LV)) % F; xs[q, g, :, :, z] = x0[:, :, z]
    return pack(th, su, st, xs, hv)
def setup_inputs_ends(rng):
    kind = rng.integers(0, 4, (N, 8, 1, F)); mix = rng.integers(0, 2, (N, 8, 16, F)); i = np.arange(16)
    th = 4095 * np.where(kind == 0, 0, np.where(kind == 1, 1, mix))
    off = (rng.random((N, 8, 1, F)) < 0.25) & (i[:, None] == rng.integers(0, 16, (N, 8, 1, F))); th = np.where(off, np.abs(th - 1), th)
    th[..., [0, 1, 4]] = 0; th[..., [F - 1, F - 2, 2]] = 4095; th[:, :, 15, 1] = 1; th[:, :, 15, F - 2] = 4094
    e = rng.random((N, 8, 16, F)); su = np.where(e < 0.35, 0, np.where(e < 0.7, F - 1, rng.integers(0, F, e.shape)))
    su[..., F - 3] = np.where(i == 15, F - 2, np.where(i % 2 == 0, F - 1, 2)); su[..., 5] = np.where(i == 15, 1, np.where(i % 2 == 0, 4, 0))
    su[..., 3] = np.where(i % 2 == 0, F - 1, 2); su[..., 7] = np.where(i % 2 == 0, 4, 0)
    e = rng.random((N, 8, LV, S)); st = np.where(e < 0.35, 0, np.where(e < 0.7, F - 1, rng.integers(0, F, e.shape)))
    kind = rng.integers(0, 4, (N, 8, 1, T, S)); mix = rng.integers(0, 2, (N, 8, 16, T, S)); xs = 4095 * np.where(kind == 0, 0, np.where(kind == 1, 1, mix))
    for j, a, x in ((1, F - 3, 0), (2, 5, 4095), (3, 3, 0), (4, 7, 0)): st[..., S - j] = a; xs[..., S - j] = x
    hv = np.where(rng.random((N, 8, 16, 16)) < 0.5, 0.25, 2.0)
    return pack(th, su, st, xs, hv)
def setup_inputs_spread(rng):
    th, su, st, xs, hv = parts(rng)
    def uneven(n, shape, own):
        return np.minimum((n * np.power(rng.random(shape), np.exp2(rng.integers(-2, 3, own)))).astype(np.int64), n - 1)
    th = uneven(4096, th.shape, (N, 8, 1, F)); xs = uneven(4096, xs.shape, (N, 8, 1, T, S))
    su = uneven(F, su.shape, (N, 8, 1, F)); st = uneven(F, st.shape, (N, 8, LV, S))
    hv = (1 + rng.random((N, 8, 16, 16))) * np.exp2(rng.integers(-2, 1, (N, 8, 1, 16)))
    return pack(th, su, st, xs, hv)
def setup_inputs_ties(rng):
    th, su, st, xs, hv = parts(rng); m = F // 8
    for q in range(N):
        for g in range(8):
            base = rng.integers(0, 4093, (16, 8)); base[:, 0] = 0; base[:, 1] = 4092; pat = rng.integers(0, 4, (16, 8, 12))
            o = rng.permutation(F)[:8 * m].reshape(8, m); fam = rng.integers(0, 8, F); fam[o] = np.arange(8)[:, None]
            th[q, g] = base[:, fam] + pat[:, fam, rng.integers(0, 12, F)]
            su[q, g] = o[rng.integers(0, 8, F)[None, :], rng.integers(0, m, (16, F))]
            fs = rng.integers(0, 8, S); fs[0] = 0; fs[S - 1] = 1
            close = base[:, fs][:, None, :] + rng.integers(0, 4, (16, T, S))
            keep = (rng.random(S) < 0.6) | (fs < 2); xs[q, g] = np.where(keep[None, None, :], close, xs[q, g])
    st = rng.integers(0, F, st.shape)
    return pack(th, su, st, xs, hv)
def check_ranges(d):
    bad = []
    for k, lo, hi in (("th", 0, 4095), ("su", 0, F - 1), ("st", 0, F - 1), ("xs", 0, 4095), ("hv", 0.25, 2.0)):
        a = np.asarray(d[k]).astype(np.float64)
        if not (np.min(a) >= lo and np.max(a) <= hi): bad.append("range of " + k)
    return bad
def pick(A, ix):
    return np.stack([np.stack([np.take(A[q, g], ix[q, g], axis=1) for g in range(8)]) for q in range(N)])
def members(P, names):
    return pick(P, np.ascontiguousarray(names.transpose(0, 1, 3, 2)).reshape(N, 8, S * 16)).reshape(N, 8, 16, S, 16)
def reference(th, su, st, xs, hv):
    P = np.zeros((N, 8, 16, W), np.int64); P[..., :F] = th.reshape(N, 8, 16, F)
    U = np.zeros((N, 8, 16, W), np.int64); U[..., :F] = su.reshape(N, 8, 16, F)
    x = xs.astype(np.int64).reshape(N, 8, 16, T, S); first = np.stack([gentries(a) for a in st]).astype(np.int64).reshape(N, 8, LV, S)
    opener = [first[:, :, l] for l in range(LV)]; cand = [pick(U, a) for a in opener]
    X = [np.zeros((N, 8, 16, S), np.int64) for l in range(LV)]; kids = [np.ones((N, 8, 16, S)) for l in range(LV)]
    ym = []; m = 0
    for t in range(1, T + 1):
        for l in range(LV): X[l] = X[l] + x[:, :, :, t - 1]
        for l in range(LV):
            L = LN[l]
            if t % L != 0: continue
            D = np.abs(L * members(P, cand[l]) - X[l][..., None])
            M = np.add.reduce(np.exp(D * -(2.0 ** -(9 + SH[l]))), axis=-1) * 2.0 ** -4
            if l > 0: M = 0.5 * M + 0.5 * kids[l]
            ym.append(M)
            win = np.argmin(np.add.reduce(D, axis=2), axis=-1)
            b = np.take_along_axis(cand[l], win[:, :, None, :], 2)[:, :, 0]
            new = (3 * L * pick(P, b) + X[l]) >> (2 + SH[l])
            n0 = F + m * S
            for q in range(N):
                for g in range(8):
                    a, s = np.unique(opener[l][q, g], return_index=True)
                    U[q, g, m, a] = n0 + s
            col = pick(U, b)
            P[..., n0:n0 + S] = np.roll(new, l, axis=0); U[..., n0:n0 + S] = np.roll(col, l, axis=0)
            opener[l] = b; cand[l] = col; X[l] = np.zeros((N, 8, 16, S), np.int64); kids[l] = np.ones((N, 8, 16, S))
            if l + 1 < LV: kids[l + 1] = kids[l + 1] * M
            m += 1
    h = np.asarray(hv).astype(np.float64).reshape(N, 8, 16, 1, 16); yz = []
    for m in range(C):
        n0 = F + m * S
        D = np.abs(members(P, U[..., n0:n0 + S]) - P[..., n0:n0 + S][..., None])
        yz.append(np.add.reduce(h * np.exp(D * -(2.0 ** -9)), axis=-1) * 2.0 ** -4)
    return {"ym": np.concatenate(ym, axis=3).reshape(N, 128, C * S).astype(np.float32), "yz": np.concatenate(yz, axis=3).reshape(N, 128, C * S).astype(np.float32)}

def check_inputs(d):
    bad = list(check_ranges(d))
    if not bad:
        for name, y in reference(**d).items():
            for q in range(N):
                v = np.abs(np.asarray(y[q], np.float64)); s = np.sqrt(np.mean(v * v))
                if v.max() > 6 * s or s < 2.0 ** -4: bad.append('%s of rank %d is uneven or too small' % (name, q))
    return bad

@@ -1,0 +1,530 @@
+import math
+from concourse.bass import DstId, RemoteDMATransfer
+from concourse.mybir import AluOpType as A, ActivationFunctionType as AF
+
+F, S, OFF = 1984, 256, 16
+W = OFF + F + 6 * S
+
+
+def n0(m):
+    return OFF + F + m * S
+
+
+SCRATCH = {
+    "P": ("sbuf", [128, W], "int32"),
+    "sur": ("sbuf", [128, OFF + F], "int32"),
+    "U": ("sbuf", [128, n0(4)], "float32"),
+    "str": ("sbuf", [128, 32], "int32"),
+    "hvr": ("sbuf", [128, 16], "bfloat16"),
+    "lnh": ("sbuf", [128, 16], "float32"),
+    "nx": ("sbuf", [128, 4 * S], "float16"),
+    "nP": ("sbuf", [128, 6 * S], "float16"),
+    "Pg0": ("sbuf", [128, 4096], "float16"), "Pg1": ("sbuf", [128, 4096], "float16"), "Pg2": ("sbuf", [128, 4096], "float16"),
+    "A0": ("sbuf", [128, 16, 512], "float32"), "A1": ("sbuf", [128, 16, 512], "float32"),
+    "A2": ("sbuf", [128, 16, 512], "float32"), "A3": ("sbuf", [128, 16, 512], "float32"),
+    "R": ("sbuf", [128, 16 * S], "float32"),
+    "cu": ("sbuf", [128, 10 * S], "uint16"),
+    "sn": ("sbuf", [128, 2 * S], "int32"),
+    "obu": ("sbuf", [128, 8 * 16], "uint16"), "obf": ("sbuf", [128, 8 * 16], "float32"), "obh": ("sbuf", [128, 8 * 16], "float16"),
+    "so": ("sbuf", [128, 32], "uint16"),
+    "e1": ("sbuf", [128, S], "float32"), "e2": ("sbuf", [128, S], "float32"), "e3": ("sbuf", [128, S], "float32"),
+    "e4": ("sbuf", [128, S], "float32"), "e5": ("sbuf", [128, S], "float32"),
+    "ua": ("sbuf", [128, S], "float32"), "sm": ("sbuf", [128, 32], "float32"), "ru": ("sbuf", [128, 48], "uint16"),
+    "Nm": ("sbuf", [128, 6 * S], "float32"), "Dm": ("sbuf", [128, 15 * 128], "bfloat16"),
+    "I32": ("sbuf", [128, 128], "float32"), "Ib": ("sbuf", [128, 4 * 128], "bfloat16"),
+    "jr": ("sbuf", [128, S], "float32"), "dl": ("sbuf", [128, S], "float32"), "big": ("sbuf", [128, S], "float32"),
+    "one": ("sbuf", [128, S], "float32"), "dmk": ("sbuf", [128, S], "bfloat16"), "slr": ("sbuf", [128, S], "bfloat16"),
+    "blk": ("sbuf", [128, 16], "float32"), "ci": ("sbuf", [128, 32], "int32"), "cfl": ("sbuf", [128, 16], "float32"),
+    "bco": ("sbuf", [128, 16], "uint16"), "rdo": ("sbuf", [128, 4], "uint16"),
+    "ps": ("psum", [128, 4096], "float32"),
+}
+FOLD = [(0, 512), (512, 1024), (1024, 1536), (1536, 2048), (2048, 2560), (2560, 3072)]
+NFOLD = len(FOLD)
+NARROW = (0, 2)
+SEMAPHORES = (["pe", "act", "dve", "pool", "hl"] + ["d%d" % k for k in range(16)] + ["l%d" % k for k in range(12)]
+              + ["f%d" % k for k in range(NFOLD)] + ["b%d" % k for k in range(NFOLD)] + ["a%d" % k for k in range(5)])
+LODGE = {"xa": ("P", n0(0)), "xb": ("P", n0(3)), "Pr": ("nx", 0), "cf": ("R", 3328), "TT": ("Nm", 0), "t1": ("e1", 0), "pr": ("e2", 0)}
+ON_VECTOR = ("r5u1", "r5u2", "r5u3")
+WOVEN = ((0, "c2", 0), (1, "c2", 1), (2, "c3", 1), (3, "c5", 0), (4, "c5", 1), (5, "r2", 0))
+ORDER = """
+load first1 u0 first0 u1 c0g0 x0 c0u1 twins0 c0g1 c0u0 c0u2 firstf0 prep0 c0s0 c0u3 c0s1 c0e0 ext0 c0s2 c0s3 c2u0 elect0 firstf1 c2u1 won0 snap0 keep0 prep2 col0 neg0 c2s0 c0e2 c0e3 place0 c1g0 prep1 c1u0 c1u1 twins1 c1s0 c1g1 c1u2 c1u3 c1s1 c1s2 c2e0 c0e1 c1s3 c2s1 c2e1 ext1 r0u0 c1e0 c2u2 elect1 c2u3 x1 won1 snap1 c2s2 c2s3 col1 keep1 c2e2 c2e3 r0u2 r0u1 c3g0 twins2 elect2 r0e0 c1e1 neg1 place1 won2 snap2 r0e2 c3u0 prep3 r0e1 c3u1 c3s0 c1e3 r0u3 ext2 twins3 fold0 col2 c3s1 c3e1 send0 c3u3 c3u2 r1u0 c3s2 ext3 c1e2 r1u2 c3s3 c3e0 r0e3 r1u1 c5u0 elect3 place2 prep5 r1e0 send1 c3e3 won3 snap3 keep3 col3 place3 c3e2 r1u3 c5u1 c5s0 c4g0 prep4 r1e2 c4g1 send2 c4u1 c4u0 r1e1 twins4 c4u2 c4u3 c4s0 c4e0 c4s1 c4s2 c5s1 r1e3 ext4 c4s3 neg3 c5e0 c4e1 keep2 fold1 c4e3 c5u2 c5e1 c5u3 elect4 c4e2 twins5 c5s2 fold3 c5s3 c5e2 c5e3 ym0 r2g1 won4 neg2 r3u1 r2u2 r3e1 r3u2 col4 r3u0 r3e2 fold2 ext5 r3e0 r2u0 r3u3 elect5 snap4 won5 col5 r2e0 snap5 r2u1 r4g0 r2e1 r2u3 neg4 r4u0 send4 r4g1 lists r2e2 gagain r2e3 send3 r4u1 r3e3 r4u3 fold4 r5g0 neg5 again fold5 ym3 r4u2 r5u0 r5g1 r5u1 r5u2 ym4 r4e0 r4e1 r5u3 r4e2 upper2 yz2 ym1 last0 r4e3 last1 yz4 upper5 last2 yz0 last3
+""".split()
+
+
+def helper_of(core, T, topo):
+    near = [c for c in topo.cores_of(core) if c != core and T.rank_of(c) is None and topo.die(c) == topo.die(core)]
+    return min(near, key=lambda c: abs(c - core))
+
+
+def fold_mask(k, core, T, topo):
+    mk = topo.mask(core, helper_of(core, T, topo))
+    return mk & ~topo.mask(core, T.cores[(T.rank_of(core) + 1) % len(T.cores)]) if k in NARROW else mk
+
+
+def bits(m):
+    return bin(m).count("1")
+
+
+def rank_program(g, core, T, topo):
+    rank = T.rank_of(core)
+    if rank is None:
+        for owner in T.cores:
+            if helper_of(owner, T, topo) == core:
+                rid, pid = topo.addr(owner)[:2]
+                m_out = topo.mask(core, owner)
+                for k in [int(t[4:]) for t in ORDER if t[:4] == "fold"]:
+                    lo, hi = FOLD[k]
+                    g.wait_ge(T.sem["f%d" % k], bits(fold_mask(k, owner, T, topo)))
+                    g.remote_dma(T.R[:, lo:hi], T.R[:, lo:hi], T.sem["b%d" % k], T.sem.hl, pid, rid, m_out)
+                g.wait_ge(T.sem.hl, NFOLD * bits(m_out))
+        return
+    N = len(T.cores)
+    nxt, prv, hlp = T.cores[(rank + 1) % N], T.cores[(rank - 1) % N], helper_of(core, T, topo)
+    ops = []
+
+    def v(name, lo=None, hi=None, step=1):
+        if name in LODGE:
+            name, lo, hi = LODGE[name][0], LODGE[name][1] + lo, LODGE[name][1] + hi
+        t = T[name]
+        if lo is None:
+            lo, hi = 0, t.shape[1]
+        if name == "ps":
+            reg = [("ps", b, b + 1, lo, hi) for b in range(lo // 512, (hi - 1) // 512 + 1)]
+        else:
+            reg = [(name, lo, hi)]
+        return (t[:, lo:hi] if step == 1 else t[:, lo:hi:step], reg)
+
+    def v3(name, i0, i1, lo, hi):
+        reg = [(name, i * 512 + lo, i * 512 + hi) for i in range(i0, i1)]
+        return (T[name][:, i0, lo:hi] if i1 == i0 + 1 else T[name][:, i0:i1, lo:hi], reg)
+
+    def ind(win, off):
+        return (win[0].indirect(off[0]), win[1], off[1])
+
+    def op(q, fn, reads, writes, sem=None, inc=1):
+        rr, ww = [], []
+        for x in reads:
+            if isinstance(x, tuple):
+                rr += x[1] + (x[2] if len(x) > 2 else [])
+        for x in writes:
+            ww += x[1]
+            rr += x[2] if len(x) > 2 else []
+        ops.append({"q": q, "fn": fn, "r": rr, "w": ww, "sem": sem, "inc": inc})
+
+    def val(x):
+        return x[0] if isinstance(x, tuple) else x
+
+    def mm(out, l, r, start, stop):
+        op("pe", lambda: g.tensor.matmul(out[0], l[0], r[0], start, stop), [l, r], [out])
+
+    def cp(out, a):
+        op("dve", lambda: g.vector.tensor_copy(out[0], a[0]), [a], [out])
+
+    def tt(out, a, b, o):
+        op("dve", lambda: g.vector.tensor_tensor(out[0], a[0], b[0], o), [a, b], [out])
+
+    def ts(out, a, s1, o0, s2=None, o1=None):
+        if o1 is None:
+            op("dve", lambda: g.vector.tensor_scalar(out[0], a[0], val(s1), None, o0), [a, s1], [out])
+        else:
+            op("dve", lambda: g.vector.tensor_scalar(out[0], a[0], val(s1), val(s2), o0, o1), [a, s1, s2], [out])
+
+    def scan(out, d0, d1, o0, o1):
+        op("dve", lambda: g.vector.tensor_tensor_scan(out[0], d0[0], d1[0], 0.0, o0, o1), [d0, d1], [out])
+
+    def turn(out, a):
+        op("dve", lambda: g.vector.transpose(out[0], a[0]), [a], [out])
+
+    def fill(out, c):
+        op("dve", lambda: g.vector.memset(out[0], c), [], [out])
+
+    def act(out, a, f, bias=0.0, scale=1.0):
+        op("act", lambda: g.scalar.activation(out[0], a[0], f, bias=val(bias), scale=val(scale)), [a, bias, scale], [out])
+
+    def iota(out, pat, base, cm, flt):
+        if flt:
+            op("pool", lambda: g.iota(out[0], pat, base, cm, allow_small_or_imprecise_dtypes=True), [], [out])
+        else:
+            op("pool", lambda: g.iota(out[0], pat, base, cm), [], [out])
+
+    def sel(out, a, pat, cmp, fl):
+        op("pool", lambda: g.affine_select(out[0], a[0], pat, cmp, fl, 0, 1), [a], [out])
+
+    nd, nl = [0], [0]
+
+    def dma(q, out, a):
+        e = g.sync if q == "sp" else g.scalar
+        op(q, lambda: e.dma_start(out[0], a[0]), [a], [out], sem="d%d" % nd[0], inc=16)
+        nd[0] += 1
+
+    def hbm(t):
+        return (t, [])
+
+    def send(k, out, a):
+        rid, pid = topo.addr(nxt)[:2]
+        mk, ls = topo.mask(core, nxt), "l%d" % nl[0]
+        nl[0] += 1
+        op("pool", lambda: g.remote_dma(out[0], a[0], T.sem["a%d" % k], T.sem[ls], pid, rid, mk), [a], [], sem=ls, inc=-bits(mk))
+        op("far", None, [], [out], sem="a%d" % k, inc=bits(topo.mask(prv, core)))
+
+    def fold(k, srcs):
+        rid, pid = topo.addr(hlp)[:2]
+        mk, ls = fold_mask(k, core, T, topo), "l%d" % nl[0]
+        nl[0] += 1
+        out = v("R", *FOLD[k])
+        op("pool", lambda: g.remote_dma_fused([RemoteDMATransfer(
+            dst_ids=[DstId(rid=rid, pnc=pid)], dma_engine_mask=mk, remote_sem=T.sem["f%d" % k],
+            srcs=[s[0] for s in srcs], dsts=[out[0]], alu_op=1)], local_sem=T.sem[ls]), srcs, [], sem=ls, inc=-bits(mk))
+        op("far", None, [], [out], sem="b%d" % k, inc=bits(topo.mask(hlp, core)))
+
+    LEVEL = [0, 0, 1, 0, 0, 1]
+    TIMES = [[0], [1], [0, 1], [2], [3], [2, 3]]
+    CAND = [0, 2, 1, 3, 5, 4]
+    RCU = [2, 3, 8, 5, 6, 9]
+    NWIN = [n0(0), n0(1), n0(0), n0(2), n0(4), n0(3)]
+    XWIN = [n0(0), n0(0), n0(0), n0(2), n0(2), n0(0)]
+    PG = {"c0": "Pg0", "c2": "Pg1", "c1": "Pg2", "c3": "Pg0", "c4": "Pg1", "c5": "Pg2", "r2": "Pg0", "r4": "Pg1", "r5": "Pg2",
+          "r0": "Pg2", "r1": "Pg0", "r3": "Pg1"}
+    AB = {"c0": ("A0", 0), "c2": ("A0", S), "c1": ("A1", 0), "c3": ("A1", S), "r0": ("A2", 0), "r1": ("A2", S),
+          "c5": ("A3", 0), "c4": ("A3", S), "r2": ("A0", 0), "r3": ("A0", S), "r4": ("A1", 0), "r5": ("A1", S)}
+    I1, IH, IQ, IE = (v("Ib", k * 128, k * 128 + 128) for k in range(4))
+    qf = v("cfl", 0, 1)
+    dbuf = [0]
+    KEY, XQ, EL, TW = [2048, 3584], [2560, 2816], [3072, 3088], 3328
+
+    def ring():
+        dbuf[0] ^= 1
+        return dbuf[0] * 1024
+
+    def cut(k, lo=0, hi=S):
+        return v("cu", k * S + lo, k * S + hi)
+
+    def ob(kind, k):
+        return v("ob" + kind, k * 16, k * 16 + 16)
+
+    def cand_f(m, lo, hi):
+        if m in (0, 2, 5):
+            k = {0: 0, 2: 1, 5: 2}[m]
+            return v("cf", k * S + lo, k * S + hi)
+        b = n0({1: 0, 3: 1, 4: 3}[m])
+        return v("U", b + lo, b + hi)
+
+    def load():
+        dma("sp", v("str"), hbm(T.st[:]))
+        dma("sp", v("sur", OFF, OFF + F), hbm(T.su[:]))
+        dma("act", v("P", OFF, OFF + F), hbm(T.th[:]))
+        dma("sp", v("xa", 0, 512), hbm(T.xs[:, 0:512]))
+        dma("act", v("hvr"), hbm(T.hv[:]))
+        dma("sp", v("xb", 0, 512), hbm(T.xs[:, 512:1024]))
+        fill(v("I32"), 1.0)
+        fill(v("Dm"), -1.0)
+        fill(v("P", 0, OFF), 0)
+        fill(v("sur", 0, OFF), 0)
+        fill(v("U", 0, OFF), 0.0)
+        iota(v("ci", 0, 1), [[0, 1]], 0, 1, False)
+        iota(v("jr"), [[0, 16], [1, 16]], 0, 0, True)
+        sel(v("I32"), v("I32"), [[-1, 128]], A.is_equal, 0.0)
+        iota(v("ci", 16, 32), [[16, 16]], 15, 0, False)
+        iota(v("Nm"), [[1, 6 * S]], n0(0), 0, True)
+        sel(v("Dm"), v("Dm"), [[0, 15], [-16, 8], [-1, 16]], A.is_equal, 0.0)
+        sel(v("Dm"), v("Dm"), [[-1, 15], [-16, 8], [0, 16]], A.not_equal, 1.0)
+        ts(v("ci", 1, 2), v("ci", 0, 1), 15, A.bitwise_and)
+        ts(v("ci", 2, 3), v("ci", 0, 1), 4, A.logical_shift_right)
+        ts(v("big"), v("jr"), 0.0, A.is_equal, 2.0 ** 40, A.mult)
+        cp(v("cfl", 0, 2), v("ci", 1, 3))
+        tt(v("ci", 3, 4), v("ci", 0, 1), v("ci", 2, 3), A.add)
+        ts(v("one"), v("jr"), 0.0, A.is_equal)
+        ts(v("ci", 4, 5), v("ci", 3, 4), 1, A.bitwise_and)
+        ts(v("dl"), v("jr"), qf, A.is_equal)
+        ts(v("cfl", 2, 3), v("ci", 4, 5), 33.0, A.mult, qf, A.add)
+        ts(v("dmk"), v("jr"), qf, A.is_gt, 64.0, A.mult)
+        for k, c in enumerate((3.0, 4.0, 260.0)):
+            ts(v("rdo", k, k + 1), v("cfl", 2, 3), 16.0, A.mult, c, A.add)
+        ts(v("blk", 0, 8), v("jr", 0, 8), v("cfl", 1, 2), A.is_equal)
+        ts(v("blk", 8, 16), v("jr", 0, 8), v("cfl", 1, 2), A.is_equal, 2.0 ** 17, A.mult)
+        cp(v("bco"), v("ci", 16, 32))
+        ts(v("obu", 0, 32), v("str"), float(OFF), A.add)
+        ts(v("obf", 0, 32), v("str"), float(OFF), A.add)
+        ts(v("obh", 0, 32), v("str"), float(OFF - 2048), A.add, 2.0 ** -6, A.mult)
+        for k, c in enumerate((1.0, 0.5, -0.25, -0.125)):
+            act(v("Ib", k * 128, k * 128 + 128), v("I32"), AF.Copy, scale=c)
+        act(v("slr"), v("jr"), AF.Copy, scale=4096.0)
+        act(v("lnh"), v("hvr"), AF.Ln, scale=1.0 / 16)
+        for m in range(6):
+            act(v("Nm", m * S, m * S + S), v("Nm", m * S, m * S + S), AF.Copy, scale=v("dl", m, m + 1))
+
+    def first(k):
+        ts(cut(k), ind(v("sur"), ob("u", k)), float(OFF), A.add)
+
+    def conv_u(lo, hi):
+        ts(v("U", lo, hi), v("sur", lo, hi), float(OFF), A.add)
+
+    def conv_x(k):
+        ts(v("nx", k * 512, k * 512 + 512), v("xb" if k else "xa", 0, 512), -1.0, A.mult, 2048.0, A.add)
+
+    def neg_p(m):
+        ts(v("nP", m * S, m * S + S), v("P", n0(m), n0(m) + S), -1.0, A.mult, 2048.0, A.add)
+
+    def gather(name, h, parts=1):
+        m, n = int(name[1]), 128 // parts
+        k, w = (CAND[m], NWIN[m]) if name[0] == "c" else (RCU[m], n0(m + 1))
+        for s in range(h * 128, h * 128 + 128, n):
+            ts(v(PG[name], s * 16, (s + n) * 16), ind(v("P", 0, w), cut(k, s, s + n)), -2048.0, A.add)
+
+    def prep(m):
+        kb, tm = KEY[LEVEL[m]], TIMES[m]
+        for h in range(2):
+            mm(v("ps", kb + S + h * 128, kb + S + h * 128 + 128), cand_f(m, h * 128, h * 128 + 128), v("I32"), True, True)
+        for k, t in enumerate(tm):
+            mm(v("ps", XQ[LEVEL[m]], XQ[LEVEL[m]] + S), IQ if len(tm) == 1 else IE, v("nx", t * S, t * S + S), k == 0, k == len(tm) - 1)
+        mm(v("ps", kb, kb + S), I1, v("slr"), True, False)
+
+    def unit(name, u):
+        m, h, b = int(name[1]), u // 2, ring()
+        subs = [("nx", t) for t in TIMES[m]] if name[0] == "c" else [("nP", m)]
+        for j in range(8):
+            o = v("ps", b + j * 128, b + j * 128 + 128)
+            mm(o, I1, v(PG[name], h * 2048 + (u % 2) * 8 + j, h * 2048 + 2048, 16), True, False)
+            for k, (t, c) in enumerate(subs):
+                mm(o, I1 if len(subs) == 1 else IH, v(t, c * S + h * 128, c * S + h * 128 + 128), False, k == len(subs) - 1)
+        an, ao = AB[name]
+        x = v3(an, (u % 2) * 8, (u % 2) * 8 + 8, ao + h * 128, ao + h * 128 + 128)
+        if "%su%d" % (name, u) in ON_VECTOR:
+            ts(x, v("ps", b, b + 1024), -1.0, A.mult)
+            tt(x, v("ps", b, b + 1024), x, A.max)
+        else:
+            act(x, v("ps", b, b + 1024), AF.Abs)
+
+    def score(m, u):
+        an, ao = AB["c%d" % m]
+        h, kb = u // 2, KEY[LEVEL[m]]
+        for j in range(8):
+            i = (u % 2) * 8 + j
+            mm(v("ps", kb + h * 128 + i, kb + h * 128 + 128, 16), v3(an, i, i + 1, ao + h * 128, ao + h * 128 + 128), v("blk", 8, 16),
+               False, u == 3 and j == 7)
+
+    def exp_c(m, u):
+        an, ao = AB["c%d" % m]
+        x = v3(an, (u % 2) * 8, (u % 2) * 8 + 8, ao + (u // 2) * 128, ao + (u // 2) * 128 + 128)
+        act(x, x, AF.Exp, bias=-math.log(16.0 * (1 + LEVEL[m])), scale=-1.0 / 512)
+
+    def unit_r(m, slots):
+        name, b = "r%d" % m, ring()
+        for j, i in enumerate(slots):
+            o = v("ps", b + j * S, b + j * S + S)
+            mm(o, I1, v(PG[name], i, 4096, 16), True, False)
+            mm(o, I1, v("nP", m * S, m * S + S), False, True)
+        an, ao = AB[name]
+        act(v3(an, slots[0], slots[-1] + 1, ao, ao + S), v("ps", b, b + len(slots) * S), AF.Abs)
+
+    def exp_r(an, slots, lo, hi):
+        for i in slots:
+            x = v3(an, i, i + 1, lo, hi)
+            act(x, x, AF.Exp, bias=v("lnh", i, i + 1), scale=-1.0 / 512)
+
+    def elect(m):
+        kb, el = KEY[LEVEL[m]], EL[LEVEL[m]]
+        key = v("ps", kb, kb + S)
+        scan(v("e1"), v("big"), key, A.add, A.min)
+        tt(v("e2"), key, v("e1"), A.subtract)
+        tt(v("e3"), v("ps", kb + S, kb + 2 * S), v("e2"), A.subtract)
+        scan(v("e4"), v("e2"), v("e3"), A.min, A.max)
+        tt(v("e5"), ind(v("e4"), v("bco")), v("dl"), A.mult)
+        for h in range(2):
+            mm(v("ps", el + h * 8, el + h * 8 + 8), v("e5", h * 128, h * 128 + 128), v("blk", 0, 8), True, True)
+
+    def won(m):
+        cp(ob("u", 2 + m), v("ps", EL[LEVEL[m]], EL[LEVEL[m]] + 16))
+
+    def keep(m):
+        el = EL[LEVEL[m]]
+        act(ob("f", 2 + m), v("ps", el, el + 16), AF.Copy)
+        ts(ob("h", 2 + m), ob("u", 2 + m), -2048.0, A.add, 2.0 ** -6, A.mult)
+
+    def snap(m):
+        ts(v("t1", 0, S), ind(v("P", 0, NWIN[m]), ob("u", 2 + m)), 0.75, A.mult, 512.0 - (0.375 if LEVEL[m] == 0 else 0.4375), A.add)
+        out = v("P", n0(m), n0(m) + S) if LEVEL[m] == 0 else v("sn", (m // 3) * S, (m // 3) * S + S)
+        tt(out, v("ps", XQ[LEVEL[m]], XQ[LEVEL[m]] + S), v("t1", 0, S), A.add)
+
+    def column(m):
+        cp(cut(2 + m), ind(v("U", 0, NWIN[m]), ob("u", 2 + m)))
+
+    def place(m):
+        cp(v("U", n0(m), n0(m) + S) if LEVEL[m] == 0 else v("cf", 2 * S, 3 * S), cut(2 + m))
+
+    def twins(m):
+        mm(v("ps", TW, TW + S), I1, v("dmk"), True, False)
+        for j in range(15):
+            mm(v("ps", TW + j + 1, TW + S, 16), v("Dm", j * 128, j * 128 + 128), ob("h", CAND[m]), False, j == 14)
+
+    def extend(m):
+        scan(v("pr", 0, S), v("ps", TW, TW + S), v("one"), A.mult, A.add)
+        if m in (0, 1, 4):
+            src = [cand_f(m, c * 16, c * 16 + 16) for c in range(16)]
+        else:
+            cp(v("ua"), ind(v("U", 0, XWIN[m]), ob("u", CAND[m])))
+            src = [v("ua", c * 16, c * 16 + 16) for c in range(16)]
+        ts(v("sm", 0, 16), v("pr", 15, S, 16), 0.0, A.not_equal)
+        tt(v("sm", 16, 32), v("sm", 0, 16), ob("f", CAND[m]), A.mult)
+        ts(v("so", 0, 32, 2), v("sm", 16, 32), qf, A.max)
+        for c in range(15, -1, -1):
+            tt(ind(v("U", 0, XWIN[m]), v("so", 2 * c, 2 * c + 1)), src[c], v("Nm", m * S + c * 16, m * S + c * 16 + 16), A.max)
+
+    def again_lists():
+        b = n0(0)
+        turn(v("TT", 0, 512), v("U", b, b + 512))
+        turn(v("TT", 512, 1056), v("U", b - 16, b + 528))
+        cp(v("ru"), ind(v("TT", 0, 1056), v("rdo", 0, 3)))
+
+    def again():
+        b = ring()
+        for j, m in enumerate((0, 0, 1)):
+            o = v("ps", b + j * S, b + j * S + S)
+            mm(o, I1, v("Pr", j * S, j * S + S), True, False)
+            mm(o, I1, v("nP", m * S, m * S + S), False, True)
+        act(v3("A2", 3, 4, 0, S), v("ps", b, b + S), AF.Abs)
+        act(v3("A2", 4, 5, 0, 2 * S), v("ps", b + S, b + 3 * S), AF.Abs)
+        x = v3("A2", 3, 4, 0, S)
+        act(x, x, AF.Exp, bias=v("lnh", 3, 4), scale=-1.0 / 512)
+        exp_r("A2", [4], 0, 2 * S)
+
+    def upper(m, a, b, q):
+        p = ring()
+        x, o = v("ps", p, p + S), 3584 + (m // 3) * S
+        act(x, v("R", a, a + S), AF.Copy, scale=0.5)
+        tt(x, x, v("R", b, b + S), A.mult)
+        tt(v("R", o, o + S), x, v("R", q, q + S), A.add)
+        dma("sp", hbm(T.ym[:, m * S:m * S + S]), v("R", o, o + S))
+
+    def out(t, m, c, n=1):
+        dma("sp", hbm(t[:, m * S:(m + n) * S]), v("R", c, c + n * S))
+
+    def slots(an, lo, hi, skip=()):
+        return [v3(an, i, i + 1, lo, hi) for i in range(16) if i not in skip]
+
+    def sum4(k):
+        for i in range(4 * k, 4 * k + 4):
+            exp_r("A1", [i], 0, S)
+            mm(v("ps", KEY[0], KEY[0] + S), v("I32"), v3("A1", i, i + 1, 0, S), i == 0, i == 15)
+
+    def out4():
+        cp(v("R", 3072, 3328), v("ps", KEY[0], KEY[0] + S))
+        out(T.yz, 4, 3072)
+
+    def last(k):
+        for i in range(4 * k, 4 * k + 4):
+            x, acc = v3("A1", i, i + 1, S, 2 * S), v("ps", KEY[1], KEY[1] + S)
+            exp_r("A1", [i], S, 2 * S)
+            if i % 2 == 0:
+                mm(v("ps", XQ[0], XQ[0] + S), v("I32"), x, i == 0, i == 14)
+            elif i == 1:
+                cp(acc, x)
+            else:
+                tt(acc if i < 15 else v("e1"), acc, x, A.add)
+        if k == 3:
+            tt(v("R", 3328, 3584), v("ps", XQ[0], XQ[0] + S), v("e1"), A.add)
+            dma("act", hbm(T.yz[:, 5 * S:6 * S]), v("R", 3328, 3584))
+
+    Q4 = [[0, 1, 2, 3], [4, 5, 6, 7], [8, 9, 10, 11], [12, 13, 14, 15]]
+    Q0 = [[0, 1, 2], [5, 6, 7, 8], [9, 10, 11, 12], [13, 14, 15]]
+    Q1 = [[0, 1, 2, 3]] + Q0[1:]
+    piece = {"load": (load,), "u0": (conv_u, OFF, 1008), "u1": (conv_u, 1008, OFF + F), "x0": (conv_x, 0), "x1": (conv_x, 1),
+             "lists": (again_lists,), "gagain": (ts, v("Pr", 0, 768), ind(v("P", 0, n0(5)), v("ru")), -2048.0, A.add), "again": (again,),
+             "send0": (send, 0, v("P", n0(2), n0(3)), v("sn", 0, S)), "send1": (send, 1, cut(8), cut(4)),
+             "send2": (send, 2, v("U", n0(2), n0(3)), v("cf", 2 * S, 3 * S)), "send3": (send, 3, cut(9), cut(7)),
+             "send4": (send, 4, v("P", n0(5), n0(6)), v("sn", S, 2 * S)),
+             "fold0": (fold, 0, slots("A0", 0, 512)), "fold1": (fold, 1, slots("A1", 0, 512)), "fold2": (fold, 2, slots("A3", 0, 512)),
+             "fold3": (fold, 3, slots("A2", 0, 512, (3, 4))), "fold4": (fold, 4, slots("A0", 0, 512)),
+             "fold5": (fold, 5, [v("R", *FOLD[3])] + [v3("A2", i, i + 1, 0, 512) for i in (3, 4)]),
+             "upper2": (upper, 2, 0, 512, 256), "upper5": (upper, 5, 768, 1280, 1024),
+             "ym0": (out, T.ym, 0, 0), "ym1": (out, T.ym, 1, 512), "ym3": (out, T.ym, 3, 768), "ym4": (out, T.ym, 4, 1280),
+             "yz0": (out, T.yz, 0, 2560, 2), "yz2": (out, T.yz, 2, 2048, 2), "yz4": (out4,)}
+    for k in range(2):
+        piece["first%d" % k] = (first, k)
+        piece["firstf%d" % k] = (cp, v("cf", k * S, k * S + S), cut(k))
+    for m in range(6):
+        for nm, fn in (("prep", prep), ("elect", elect), ("won", won), ("keep", keep), ("snap", snap), ("col", column), ("place", place),
+                       ("twins", twins), ("ext", extend), ("neg", neg_p)):
+            piece["%s%d" % (nm, m)] = (fn, m)
+        for u in range(4):
+            piece["c%du%d" % (m, u)] = (unit, "c%d" % m, u)
+            piece["c%ds%d" % (m, u)] = (score, m, u)
+            piece["c%de%d" % (m, u)] = (exp_c, m, u)
+            piece["r%du%d" % (m, u)] = (unit, "r%d" % m, u) if m in (2, 4, 5) else (unit_r, m, {0: Q0, 1: Q1, 3: Q4}[m][u])
+        for h in range(2):
+            piece["c%dg%d" % (m, h)] = (gather, "c%d" % m, h)
+            piece["r%dg%d" % (m, h)] = (gather, "r%d" % m, h)
+    for u in range(4):
+        piece["r0e%d" % u] = (exp_r, "A2", Q0[u], 0, S)
+        piece["r1e%d" % u] = (exp_r, "A2", Q1[u], S, 2 * S)
+        piece["r2e%d" % u] = (exp_r, "A0", Q4[u], 0, S)
+        piece["r3e%d" % u] = (exp_r, "A0", Q4[u], S, 2 * S)
+        piece["r4e%d" % u] = (sum4, u)
+        piece["last%d" % u] = (last, u)
+
+    def woven(m, name, h):
+        a = len(ops)
+        extend(m)
+        b = len(ops)
+        gather(name, h, 16)
+        x, y = ops[a:b], ops[b:]
+        ops[a:] = x[:-16] + [o for pair in zip(y, x[-16:]) for o in pair]
+
+    for m, name, h in WOVEN:
+        piece["ext%d" % m] = (woven, m, name, h)
+    for name in ORDER:
+        piece[name][0](*piece[name][1:])
+
+    hist = {}
+    for k, o in enumerate(ops):
+        deps = set()
+        for kind, regs in (("r", o["r"]), ("w", o["w"])):
+            for e in regs:
+                name, lo, hi = e[:3]
+                for k2, kind2, lo2, hi2 in hist.get(name, ()):
+                    if lo < hi2 and lo2 < hi:
+                        o2 = ops[k2]
+                        same = o2["q"] == o["q"] and o2["sem"] is None and o["sem"] is None
+                        if name == "ps" and not same:
+                            deps.add(k2)
+                        elif "w" in (kind, kind2) and not (same and o["q"] == "pe"):
+                            deps.add(k2)
+        o["deps"] = deps if o["q"] != "far" else set()
+        for kind, regs in (("r", o["r"]), ("w", o["w"])):
+            for e in regs:
+                name, lo, hi = e[:3]
+                h = hist.setdefault(name, [])
+                if name == "ps":
+                    h[:] = [x for x in h if not (x[2] == lo and ops[x[0]]["q"] == o["q"] and (x[1] == "r" or kind == "w"))]
+                h.append((k, kind, lo, hi))
+    needed = set()
+    for o in ops:
+        needed |= o["deps"]
+    count = {}
+    for k, o in enumerate(ops):
+        if o["sem"] is not None:
+            o["done"] = (o["sem"], abs(o["inc"]))
+        elif k in needed:
+            count[o["q"]] = count.get(o["q"], 0) + 1
+            o["done"] = (o["q"], count[o["q"]])
+    queue = {"pe": g.tensor, "act": g.scalar, "dve": g.vector, "pool": g, "sp": g.sync}
+    known = {q: {} for q in queue}
+    for k, o in enumerate(ops):
+        if o["q"] == "far":
+            o["clock"] = {}
+            continue
+        kn = known[o["q"]]
+        for d in sorted(o["deps"], reverse=True):
+            s, n = ops[d]["done"]
+            if kn.get(s, 0) < n:
+                queue[o["q"]].wait_ge(T.sem[s], n)
+                kn[s] = n
+                for s2, n2 in ops[d]["clock"].items():
+                    kn[s2] = max(kn.get(s2, 0), n2)
+        o["clock"] = dict(kn)
+        ins = o["fn"]()
+        if "done" in o and o["inc"] > 0:
+            ins.then_inc(T.sem[o["done"][0]], o["inc"])
+    for o in ops:
+        if o["sem"] is not None and max(kn.get(o["sem"], 0) for kn in known.values()) < abs(o["inc"]):
+            g.wait_ge(T.sem[o["sem"]], abs(o["inc"]))

@@ -29,7 +29,7 @@ SCRATCH = {
     "so": ("sbuf", [128, 32], "uint16"),
     "e1": ("sbuf", [128, S], "float32"), "e2": ("sbuf", [128, S], "float32"), "e3": ("sbuf", [128, S], "float32"),
     "e4": ("sbuf", [128, S], "float32"), "e5": ("sbuf", [128, S], "float32"),
-    "ua": ("sbuf", [128, S], "float32"), "sm": ("sbuf", [128, 32], "float32"), "ru": ("sbuf", [128, 48], "uint16"),
+    "pr": ("sbuf", [128, S], "float32"), "ua": ("sbuf", [128, S], "float32"), "sm": ("sbuf", [128, 32], "float32"), "ru": ("sbuf", [128, 48], "uint16"),
     "Nm": ("sbuf", [128, 6 * S], "float32"), "Dm": ("sbuf", [128, 15 * 128], "bfloat16"),
     "I32": ("sbuf", [128, 128], "float32"), "Ib": ("sbuf", [128, 4 * 128], "bfloat16"),
     "jr": ("sbuf", [128, S], "float32"), "dl": ("sbuf", [128, S], "float32"), "big": ("sbuf", [128, S], "float32"),
@@ -38,16 +38,22 @@ SCRATCH = {
     "bco": ("sbuf", [128, 16], "uint16"), "rdo": ("sbuf", [128, 4], "uint16"),
     "ps": ("psum", [128, 4096], "float32"),
 }
-FOLD = [(0, 512), (512, 1024), (1024, 1536), (1536, 2048), (2048, 2560), (2560, 3072)]
+FOLD = [(0, 512), (512, 1024), (1024, 1536), (1536, 2048), (2048, 2560)]
 NFOLD = len(FOLD)
-NARROW = (0, 2)
+NARROW = (0,)
 SEMAPHORES = (["pe", "act", "dve", "pool", "hl"] + ["d%d" % k for k in range(16)] + ["l%d" % k for k in range(12)]
               + ["f%d" % k for k in range(NFOLD)] + ["b%d" % k for k in range(NFOLD)] + ["a%d" % k for k in range(5)])
-LODGE = {"xa": ("P", n0(0)), "xb": ("P", n0(3)), "Pr": ("nx", 0), "cf": ("R", 3328), "TT": ("Nm", 0), "t1": ("e1", 0), "pr": ("e2", 0)}
+LODGE = {"xa": ("P", n0(0)), "xb": ("P", n0(3)), "Pr": ("nx", 0), "cf": ("R", 3328), "TT": ("Nm", 0), "t1": ("jr", 0)}
 ON_VECTOR = ("r5u1", "r5u2", "r5u3")
 WOVEN = ((0, "c2", 0), (1, "c2", 1), (2, "c3", 1), (3, "c5", 0), (4, "c5", 1), (5, "r2", 0))
 ORDER = """
-load first1 u0 first0 u1 c0g0 x0 c0u1 twins0 c0g1 c0u0 c0u2 firstf0 prep0 c0s0 c0u3 c0s1 c0e0 ext0 c0s2 c0s3 c2u0 elect0 firstf1 c2u1 won0 snap0 keep0 prep2 col0 neg0 c2s0 c0e2 c0e3 place0 c1g0 prep1 c1u0 c1u1 twins1 c1s0 c1g1 c1u2 c1u3 c1s1 c1s2 c2e0 c0e1 c1s3 c2s1 c2e1 ext1 r0u0 c1e0 c2u2 elect1 c2u3 x1 won1 snap1 c2s2 c2s3 col1 keep1 c2e2 c2e3 r0u2 r0u1 c3g0 twins2 elect2 r0e0 c1e1 neg1 place1 won2 snap2 r0e2 c3u0 prep3 r0e1 c3u1 c3s0 c1e3 r0u3 ext2 twins3 fold0 col2 c3s1 c3e1 send0 c3u3 c3u2 r1u0 c3s2 ext3 c1e2 r1u2 c3s3 c3e0 r0e3 r1u1 c5u0 elect3 place2 prep5 r1e0 send1 c3e3 won3 snap3 keep3 col3 place3 c3e2 r1u3 c5u1 c5s0 c4g0 prep4 r1e2 c4g1 send2 c4u1 c4u0 r1e1 twins4 c4u2 c4u3 c4s0 c4e0 c4s1 c4s2 c5s1 r1e3 ext4 c4s3 neg3 c5e0 c4e1 keep2 fold1 c4e3 c5u2 c5e1 c5u3 elect4 c4e2 twins5 c5s2 fold3 c5s3 c5e2 c5e3 ym0 r2g1 won4 neg2 r3u1 r2u2 r3e1 r3u2 col4 r3u0 r3e2 fold2 ext5 r3e0 r2u0 r3u3 elect5 snap4 won5 col5 r2e0 snap5 r2u1 r4g0 r2e1 r2u3 neg4 r4u0 send4 r4g1 lists r2e2 gagain r2e3 send3 r4u1 r3e3 r4u3 fold4 r5g0 neg5 again fold5 ym3 r4u2 r5u0 r5g1 r5u1 r5u2 ym4 r4e0 r4e1 r5u3 r4e2 upper2 yz2 ym1 last0 r4e3 last1 yz4 upper5 last2 yz0 last3
+load first0 u0 firstf0 u1 c0q0 x0 prep0 c0q1 c0u0 first1 c0q3 c0u1 c0q2 twins0 c0s0 ext0a c2o3 c0u2 c0u3 ext0b ext0c c0s1 ext0d sc0a c0s2 c2o0 c0s3 c0e2 sc0b sc0c c2o2 sc0d c2o1 c0e0 sc0e c2u1 firstf1 sc0f sc0g elect0a sc0h elect0b sc0i c2u0 elect0c sc0j elect0d sc0k sc0l c0e3 elect0e sc0m x1 prep2 sc0n c0e1 won0 sc0o snap0a sc0p keep0 col0 snap0b place0
+twins1 c2s0 ext1a prep1 twins2 c2e0 c2s1 c1q1 c1q0 ext1b c1q2 c1u0 c1u1 c1s0 ext1c c1q3 c1u2 ext1d c2o4 c2o7 sc1a c2o6 sc1b c1u3 c2e1 c1s1 c2o5 sc1c c1s2 sc1d sc1e sc1f c1e2 ext2a c1s3 sc1g sc1h sc1i c1e0 sc1j elect1a sc1k elect1b sc1l neg0 sc1m elect1c c2u2 sc1n ext2c elect1d c2u3 c2s2 sc1o elect1e sc1p ext2d c2e2 ext2b c2s3 won1 c2e3 ext2e col1 snap1a place1
+r0u2 r0u1 sc2a snap1b elect2a r0u3 sc2b prep3 c3q0 c1e3 sc2c elect2b c3q1 elect2c sc2d elect2d r0u0 keep1 c3u0 twins3 sc2e elect2e r0e1 c3u1 sc2f c3o7 sc2g won2 snap2a sc2h snap2b fold0 sc2i r0e0 c3o6 c3o5 c3o4 c3s0 neg1 sc2j ext3a c3e0 sc2k keep2 c3s1 sc2l c3e1 sc2m sc2n sc2o ext3c c3u2 c3u3 c3s2 send0 sc2p ext3d r0e2 col2
+ext3e ext3b place2 c1e1 sc3a c3e2 c5o0 r1u2 c3s3 r1u0 sc3b c5o1 c3e3 r1u1 sc3c sc3d elect3a sc3e sc3f elect3b sc3g sc3h elect3c sc3i c5o2 sc3j elect3d prep5 sc3k r1e0 sc3l elect3e sc3m c5o3 r1u3 won3 sc3n send1 keep3 twins4 sc3o snap3a sc3p snap3b col3
+ext4a r1e2 c5u0 r1e3 twins5 c4q1 c5u1 c4q0 c5s0 ext4b place3 c5e0 c4q2 c4u0 ext4c c4u1 r1e1 prep4 c4q3 r0e3 ext4d send2 c4s0 c5o7 c4u2 c4u3 c4s1 sc4a r2o1 c4e1 c4s2 sc4b sc4c neg3 c4e2 r2o2 c5o6 sc4d c5o5 neg2 sc4e c5o4 c4s3 c4e3 r3u1 sc4f sc4g sc4h r2o0 c5s1 c5e1 c5u2 sc4i c5u3 elect4a ext5a fold1 ym0 sc4j sc4k c4e0 elect4b c5s2 r2q2 sc4l r2q3 ext5c sc4m elect4c elect4d c5s3 c5e2 c5e3 r3u0 elect4e r3u2 r2o3 elect5a sc4n won4 ext5d fold3 ym1 ym3 r2u0 sc4o r2u2 r3u3 snap4a sc4p ext5b col4
+r2u1 ext5e elect5b sc5a sc5b sc5c sc5d sc5e sc5f elect5c sc5g sc5h elect5d fold2 snap4b sc5i elect5e r4q1 won5 r23e0 r2u3 sc5j r23e1 sc5k sc5l neg4 sc5m snap5a sc5n snap5b r4q0 sc5o sc5p lists col5
+r23e2 r4u1 send4 r4q3 send3 r4q2 r4u0 r23e3 r4u2 gagain again r4u3 neg5 fold4 r5q0 r5q1 r5q2 yz0 r5u0 r5q3 r5u1 r5u2 r4e0 r4e1 ym4 r5u3 upper2 last0 r4e2 r4e3 upper5 last1 yz4 yz2 last2 last3
 """.split()
 
 
@@ -211,8 +217,8 @@ def rank_program(g, core, T, topo):
 
     def load():
         dma("sp", v("str"), hbm(T.st[:]))
-        dma("sp", v("sur", OFF, OFF + F), hbm(T.su[:]))
-        dma("act", v("P", OFF, OFF + F), hbm(T.th[:]))
+        dma("act", v("sur", OFF, OFF + F), hbm(T.su[:]))
+        dma("sp", v("P", OFF, OFF + F), hbm(T.th[:]))
         dma("sp", v("xa", 0, 512), hbm(T.xs[:, 0:512]))
         dma("act", v("hvr"), hbm(T.hv[:]))
         dma("sp", v("xb", 0, 512), hbm(T.xs[:, 512:1024]))
@@ -265,10 +271,10 @@ def rank_program(g, core, T, topo):
     def neg_p(m):
         ts(v("nP", m * S, m * S + S), v("P", n0(m), n0(m) + S), -1.0, A.mult, 2048.0, A.add)
 
-    def gather(name, h, parts=1):
-        m, n = int(name[1]), 128 // parts
+    def gather(name, q, quarters=1, parts=1):
+        m, n = int(name[1]), int(64 * quarters) // parts
         k, w = (CAND[m], NWIN[m]) if name[0] == "c" else (RCU[m], n0(m + 1))
-        for s in range(h * 128, h * 128 + 128, n):
+        for s in range(int(q * 64), int((q + quarters) * 64), n):
             ts(v(PG[name], s * 16, (s + n) * 16), ind(v("P", 0, w), cut(k, s, s + n)), -2048.0, A.add)
 
     def prep(m):
@@ -337,8 +343,6 @@ def rank_program(g, core, T, topo):
         cp(ob("u", 2 + m), v("ps", EL[LEVEL[m]], EL[LEVEL[m]] + 16))
 
     def keep(m):
-        el = EL[LEVEL[m]]
-        act(ob("f", 2 + m), v("ps", el, el + 16), AF.Copy)
         ts(ob("h", 2 + m), ob("u", 2 + m), -2048.0, A.add, 2.0 ** -6, A.mult)
 
     def snap(m):
@@ -365,7 +369,8 @@ def rank_program(g, core, T, topo):
             cp(v("ua"), ind(v("U", 0, XWIN[m]), ob("u", CAND[m])))
             src = [v("ua", c * 16, c * 16 + 16) for c in range(16)]
         ts(v("sm", 0, 16), v("pr", 15, S, 16), 0.0, A.not_equal)
-        tt(v("sm", 16, 32), v("sm", 0, 16), ob("f", CAND[m]), A.mult)
+        el = EL[LEVEL[m]]
+        tt(v("sm", 16, 32), ob("f", CAND[m]) if CAND[m] < 2 else v("ps", el, el + 16), v("sm", 0, 16), A.mult)
         ts(v("so", 0, 32, 2), v("sm", 16, 32), qf, A.max)
         for c in range(15, -1, -1):
             tt(ind(v("U", 0, XWIN[m]), v("so", 2 * c, 2 * c + 1)), src[c], v("Nm", m * S + c * 16, m * S + c * 16 + 16), A.max)
@@ -402,14 +407,22 @@ def rank_program(g, core, T, topo):
     def slots(an, lo, hi, skip=()):
         return [v3(an, i, i + 1, lo, hi) for i in range(16) if i not in skip]
 
-    def sum4(k):
+    def sum_t(m, k):
+        an, ao = AB["r%d" % m]
         for i in range(4 * k, 4 * k + 4):
-            exp_r("A1", [i], 0, S)
-            mm(v("ps", KEY[0], KEY[0] + S), v("I32"), v3("A1", i, i + 1, 0, S), i == 0, i == 15)
+            exp_r(an, [i], ao, ao + S)
+            mm(v("ps", KEY[0], KEY[0] + S), v("I32"), v3(an, i, i + 1, ao, ao + S), i == 0, i == 15)
 
-    def out4():
-        cp(v("R", 3072, 3328), v("ps", KEY[0], KEY[0] + S))
-        out(T.yz, 4, 3072)
+    def out_t(m, c):
+        cp(v("R", c, c + S), v("ps", KEY[0], KEY[0] + S))
+        out(T.yz, m, c)
+
+    def out01():
+        b = ring()
+        for k, x in enumerate([v("R", *FOLD[3])] + [v3("A2", i, i + 1, 0, 512) for i in (3, 4)]):
+            mm(v("ps", b, b + 512), v("I32"), x, k == 0, k == 2)
+        cp(v("R", 2560, 3072), v("ps", b, b + 512))
+        out(T.yz, 0, 2560, 2)
 
     def last(k):
         for i in range(4 * k, 4 * k + 4):
@@ -435,10 +448,9 @@ def rank_program(g, core, T, topo):
              "send4": (send, 4, v("P", n0(5), n0(6)), v("sn", S, 2 * S)),
              "fold0": (fold, 0, slots("A0", 0, 512)), "fold1": (fold, 1, slots("A1", 0, 512)), "fold2": (fold, 2, slots("A3", 0, 512)),
              "fold3": (fold, 3, slots("A2", 0, 512, (3, 4))), "fold4": (fold, 4, slots("A0", 0, 512)),
-             "fold5": (fold, 5, [v("R", *FOLD[3])] + [v3("A2", i, i + 1, 0, 512) for i in (3, 4)]),
              "upper2": (upper, 2, 0, 512, 256), "upper5": (upper, 5, 768, 1280, 1024),
              "ym0": (out, T.ym, 0, 0), "ym1": (out, T.ym, 1, 512), "ym3": (out, T.ym, 3, 768), "ym4": (out, T.ym, 4, 1280),
-             "yz0": (out, T.yz, 0, 2560, 2), "yz2": (out, T.yz, 2, 2048, 2), "yz4": (out4,)}
+             "yz0": (out01,), "yz2": (out, T.yz, 2, 2048, 2), "yz4": (out_t, 4, 3072)}
     for k in range(2):
         piece["first%d" % k] = (first, k)
         piece["firstf%d" % k] = (cp, v("cf", k * S, k * S + S), cut(k))
@@ -452,26 +464,42 @@ def rank_program(g, core, T, topo):
             piece["c%de%d" % (m, u)] = (exp_c, m, u)
             piece["r%du%d" % (m, u)] = (unit, "r%d" % m, u) if m in (2, 4, 5) else (unit_r, m, {0: Q0, 1: Q1, 3: Q4}[m][u])
         for h in range(2):
-            piece["c%dg%d" % (m, h)] = (gather, "c%d" % m, h)
-            piece["r%dg%d" % (m, h)] = (gather, "r%d" % m, h)
+            piece["c%dg%d" % (m, h)] = (gather, "c%d" % m, 2 * h, 2)
+            piece["r%dg%d" % (m, h)] = (gather, "r%d" % m, 2 * h, 2)
+        for q in range(4):
+            piece["c%dq%d" % (m, q)] = (gather, "c%d" % m, q)
+            piece["r%dq%d" % (m, q)] = (gather, "r%d" % m, q)
     for u in range(4):
         piece["r0e%d" % u] = (exp_r, "A2", Q0[u], 0, S)
         piece["r1e%d" % u] = (exp_r, "A2", Q1[u], S, 2 * S)
-        piece["r2e%d" % u] = (exp_r, "A0", Q4[u], 0, S)
-        piece["r3e%d" % u] = (exp_r, "A0", Q4[u], S, 2 * S)
-        piece["r4e%d" % u] = (sum4, u)
+        piece["r23e%d" % u] = (exp_r, "A0", Q4[u], 0, 2 * S)
+        piece["r4e%d" % u] = (sum_t, 4, u)
         piece["last%d" % u] = (last, u)
 
     def woven(m, name, h):
         a = len(ops)
         extend(m)
         b = len(ops)
-        gather(name, h, 16)
-        x, y = ops[a:b], ops[b:]
-        ops[a:] = x[:-16] + [o for pair in zip(y, x[-16:]) for o in pair]
+        gather(name, 2 * h, 2, 16)
+        ops[a:] = [o for pair in zip(ops[b:], ops[b - 16:b]) for o in pair]
+
+    def step(fn, m, k, n=1):
+        a = len(ops)
+        fn(m)
+        ops[a:] = ops[a + k:a + k + n]
 
     for m, name, h in WOVEN:
         piece["ext%d" % m] = (woven, m, name, h)
+        for k in range(5):
+            piece["elect%d%s" % (m, "abcde"[k])] = (step, elect, m, k, 3 if k == 4 else 1)
+        for k in range(4 if m in (0, 1, 4) else 5):
+            piece["ext%d%s" % (m, "abcde"[k])] = (step, extend, m, k)
+        for k in range(2):
+            piece["snap%d%s" % (m, "ab"[k])] = (step, snap, m, k)
+        for k in range(16):
+            piece["sc%d%s" % (m, "abcdefghijklmnop"[k])] = (step, extend, m, k + (4 if m in (0, 1, 4) else 5))
+        for k in range(8):
+            piece["%so%d" % (name, k)] = (gather, name, k / 2, 0.5)
     for name in ORDER:
         piece[name][0](*piece[name][1:])
 

@@ -3,58 +3,64 @@ from concourse.bass import DstId, RemoteDMATransfer
 from concourse.mybir import AluOpType as A, ActivationFunctionType as AF
 
 F, S, OFF = 1984, 256, 16
-W = OFF + F + 6 * S
+W = F + 6 * S
 
 
 def n0(m):
-    return OFF + F + m * S
+    return F + m * S
 
 
 SCRATCH = {
     "P": ("sbuf", [128, W], "int32"),
-    "sur": ("sbuf", [128, OFF + F], "int32"),
-    "U": ("sbuf", [128, n0(4)], "float32"),
+    "U": ("sbuf", [128, OFF + n0(4)], "int32"),
     "str": ("sbuf", [128, 32], "int32"),
     "hvr": ("sbuf", [128, 16], "bfloat16"),
-    "lnh": ("sbuf", [128, 16], "float32"),
+    "lnh": ("sbuf", [128, 48], "float32"),
     "nx": ("sbuf", [128, 4 * S], "float16"),
     "nP": ("sbuf", [128, 6 * S], "float16"),
     "Pg0": ("sbuf", [128, 4096], "float16"), "Pg1": ("sbuf", [128, 4096], "float16"), "Pg2": ("sbuf", [128, 4096], "float16"),
+    "mx": ("sbuf", [128, 4096], "float16"), "Pr": ("sbuf", [128, 3 * S], "float16"),
     "A0": ("sbuf", [128, 16, 512], "float32"), "A1": ("sbuf", [128, 16, 512], "float32"),
     "A2": ("sbuf", [128, 16, 512], "float32"), "A3": ("sbuf", [128, 16, 512], "float32"),
-    "R": ("sbuf", [128, 16 * S], "float32"),
+    "R": ("sbuf", [128, 14 * S], "float32"),
     "cu": ("sbuf", [128, 10 * S], "uint16"),
+    "ch": ("sbuf", [128, 2 * S], "float16"),
     "sn": ("sbuf", [128, 2 * S], "int32"),
-    "obu": ("sbuf", [128, 8 * 16], "uint16"), "obf": ("sbuf", [128, 8 * 16], "float32"), "obh": ("sbuf", [128, 8 * 16], "float16"),
+    "obu": ("sbuf", [128, 8 * 16], "uint16"), "obh": ("sbuf", [128, 6 * 16], "float16"),
     "so": ("sbuf", [128, 32], "uint16"),
     "e1": ("sbuf", [128, S], "float32"), "e2": ("sbuf", [128, S], "float32"), "e3": ("sbuf", [128, S], "float32"),
     "e4": ("sbuf", [128, S], "float32"), "e5": ("sbuf", [128, S], "float32"),
-    "pr": ("sbuf", [128, S], "float32"), "ua": ("sbuf", [128, S], "float32"), "sm": ("sbuf", [128, 32], "float32"), "ru": ("sbuf", [128, 48], "uint16"),
-    "Nm": ("sbuf", [128, 6 * S], "float32"), "Dm": ("sbuf", [128, 15 * 128], "bfloat16"),
-    "I32": ("sbuf", [128, 128], "float32"), "Ib": ("sbuf", [128, 4 * 128], "bfloat16"),
-    "jr": ("sbuf", [128, S], "float32"), "dl": ("sbuf", [128, S], "float32"), "big": ("sbuf", [128, S], "float32"),
-    "one": ("sbuf", [128, S], "float32"), "dmk": ("sbuf", [128, S], "bfloat16"), "slr": ("sbuf", [128, S], "bfloat16"),
+    "pr": ("sbuf", [128, S], "float32"), "ua": ("sbuf", [128, S], "int32"), "sm": ("sbuf", [128, 32], "float32"), "ru": ("sbuf", [128, 48], "uint16"),
+    "Nm": ("sbuf", [128, 6 * S], "int32"), "Dm": ("sbuf", [128, 15 * 128], "bfloat16"), "xd": ("sbuf", [128, 128], "bfloat16"),
+    "I32": ("sbuf", [128, 128], "float32"), "Jb": ("sbuf", [128, 128], "bfloat16"), "Ib": ("sbuf", [128, 6 * 128], "bfloat16"),
+    "jr": ("sbuf", [128, S], "float32"), "dl": ("sbuf", [128, S], "float32"), "big": ("sbuf", [128, S], "bfloat16"),
+    "one": ("sbuf", [128, S], "bfloat16"), "dmk": ("sbuf", [128, S], "bfloat16"), "c2k": ("sbuf", [128, S], "bfloat16"),
+    "hf": ("sbuf", [128, 64], "bfloat16"),
     "blk": ("sbuf", [128, 16], "float32"), "ci": ("sbuf", [128, 32], "int32"), "cfl": ("sbuf", [128, 16], "float32"),
     "bco": ("sbuf", [128, 16], "uint16"), "rdo": ("sbuf", [128, 4], "uint16"),
     "ps": ("psum", [128, 4096], "float32"),
 }
-FOLD = [(0, 512), (512, 1024), (1024, 1536), (1536, 2048), (2048, 2560)]
-NFOLD = len(FOLD)
-NARROW = (0,)
-SEMAPHORES = (["pe", "act", "dve", "pool", "hl"] + ["d%d" % k for k in range(16)] + ["l%d" % k for k in range(12)]
-              + ["f%d" % k for k in range(NFOLD)] + ["b%d" % k for k in range(NFOLD)] + ["a%d" % k for k in range(5)])
-LODGE = {"xa": ("P", n0(0)), "xb": ("P", n0(3)), "Pr": ("nx", 0), "cf": ("R", 3328), "TT": ("Nm", 0), "t1": ("jr", 0)}
-ON_VECTOR = ("r5u1", "r5u2", "r5u3")
-WOVEN = ((0, "c2", 0), (1, "c2", 1), (2, "c3", 1), (3, "c5", 0), (4, "c5", 1), (5, "r2", 0))
-ORDER = """
-load first0 u0 firstf0 u1 c0q0 x0 prep0 c0q1 c0u0 first1 c0q3 c0u1 c0q2 twins0 c0s0 ext0a c2o3 c0u2 c0u3 ext0b ext0c c0s1 ext0d sc0a c0s2 c2o0 c0s3 c0e2 sc0b sc0c c2o2 sc0d c2o1 c0e0 sc0e c2u1 firstf1 sc0f sc0g elect0a sc0h elect0b sc0i c2u0 elect0c sc0j elect0d sc0k sc0l c0e3 elect0e sc0m x1 prep2 sc0n c0e1 won0 sc0o snap0a sc0p keep0 col0 snap0b place0
-twins1 c2s0 ext1a prep1 twins2 c2e0 c2s1 c1q1 c1q0 ext1b c1q2 c1u0 c1u1 c1s0 ext1c c1q3 c1u2 ext1d c2o4 c2o7 sc1a c2o6 sc1b c1u3 c2e1 c1s1 c2o5 sc1c c1s2 sc1d sc1e sc1f c1e2 ext2a c1s3 sc1g sc1h sc1i c1e0 sc1j elect1a sc1k elect1b sc1l neg0 sc1m elect1c c2u2 sc1n ext2c elect1d c2u3 c2s2 sc1o elect1e sc1p ext2d c2e2 ext2b c2s3 won1 c2e3 ext2e col1 snap1a place1
-r0u2 r0u1 sc2a snap1b elect2a r0u3 sc2b prep3 c3q0 c1e3 sc2c elect2b c3q1 elect2c sc2d elect2d r0u0 keep1 c3u0 twins3 sc2e elect2e r0e1 c3u1 sc2f c3o7 sc2g won2 snap2a sc2h snap2b fold0 sc2i r0e0 c3o6 c3o5 c3o4 c3s0 neg1 sc2j ext3a c3e0 sc2k keep2 c3s1 sc2l c3e1 sc2m sc2n sc2o ext3c c3u2 c3u3 c3s2 send0 sc2p ext3d r0e2 col2
-ext3e ext3b place2 c1e1 sc3a c3e2 c5o0 r1u2 c3s3 r1u0 sc3b c5o1 c3e3 r1u1 sc3c sc3d elect3a sc3e sc3f elect3b sc3g sc3h elect3c sc3i c5o2 sc3j elect3d prep5 sc3k r1e0 sc3l elect3e sc3m c5o3 r1u3 won3 sc3n send1 keep3 twins4 sc3o snap3a sc3p snap3b col3
-ext4a r1e2 c5u0 r1e3 twins5 c4q1 c5u1 c4q0 c5s0 ext4b place3 c5e0 c4q2 c4u0 ext4c c4u1 r1e1 prep4 c4q3 r0e3 ext4d send2 c4s0 c5o7 c4u2 c4u3 c4s1 sc4a r2o1 c4e1 c4s2 sc4b sc4c neg3 c4e2 r2o2 c5o6 sc4d c5o5 neg2 sc4e c5o4 c4s3 c4e3 r3u1 sc4f sc4g sc4h r2o0 c5s1 c5e1 c5u2 sc4i c5u3 elect4a ext5a fold1 ym0 sc4j sc4k c4e0 elect4b c5s2 r2q2 sc4l r2q3 ext5c sc4m elect4c elect4d c5s3 c5e2 c5e3 r3u0 elect4e r3u2 r2o3 elect5a sc4n won4 ext5d fold3 ym1 ym3 r2u0 sc4o r2u2 r3u3 snap4a sc4p ext5b col4
-r2u1 ext5e elect5b sc5a sc5b sc5c sc5d sc5e sc5f elect5c sc5g sc5h elect5d fold2 snap4b sc5i elect5e r4q1 won5 r23e0 r2u3 sc5j r23e1 sc5k sc5l neg4 sc5m snap5a sc5n snap5b r4q0 sc5o sc5p lists col5
-r23e2 r4u1 send4 r4q3 send3 r4q2 r4u0 r23e3 r4u2 gagain again r4u3 neg5 fold4 r5q0 r5q1 r5q2 yz0 r5u0 r5q3 r5u1 r5u2 r4e0 r4e1 ym4 r5u3 upper2 last0 r4e2 r4e3 upper5 last1 yz4 yz2 last2 last3
-""".split()
+FOLDS = (("A0", range(16), 0, 512, 0), ("A1", range(16), 0, 512, 512), ("A2", (0, 1, 2) + tuple(range(5, 16)), 0, 512, 1024),
+         ("A3", range(16), 0, 256, 1536), ("A3", range(16), 256, 256, 1792), ("A0", range(8), 0, 512, 2048), ("A0", range(8, 16), 0, 512, 0))
+NFOLD = len(FOLDS)
+NARROW = ()
+BEHIND = {5: (3,)}
+SEMAPHORES = (["pe", "act", "dve", "pool", "hl"] + ["d%d" % k for k in range(20)] + ["l%d" % k for k in range(12)]
+              + ["f%d" % k for k in range(NFOLD)] + ["b%d" % k for k in range(NFOLD)] + ["a%d" % k for k in range(4)])
+LODGE = {"xa": ("P", n0(0)), "xb": ("P", n0(3)), "TT": ("Nm", 0), "t1": ("jr", 0), "xt2": ("nP", 3 * S), "xt5": ("Pr", 0)}
+BYTES = {"float32": 4, "int32": 4, "float16": 2, "bfloat16": 2, "uint16": 2}
+RING = (0, 1024, 2048)
+KEY = (3072, 3584)
+TAIL_PE = (0, 5, 10)
+CUT = {"c0": 4, "c1": 8, "c3": 8, "c4": 8, "r4": 8, "r5": 4, "c2": 8, "c5": 16, "r2": 16}
+PG = {"c0": "Pg0", "c2": "Pg1", "c1": "Pg2", "c3": "Pg0", "c5": "Pg1", "c4": "Pg2", "r2": "Pg0", "r4": "Pg1", "r5": "Pg0",
+      "r0": "Pg2", "r1": "Pg0", "r3": "Pg2"}
+BY_MAX = {(2, 3): (12, 16), (4, 5): (8, 16)}
+EXP_CALLS = 2
+DUE = {"sc5": -34, "size2": -19, "again": -13, "size4": -2, "fold6": 7, "max4": 35, "out": 48}
+CYCLE, PE_CYCLE, GATHER, SCATTER, CALL, WAKE, DMA_FIX, DMA_RATE = 0.83, 0.38, 1.3, 3.5, 50.0, 170.0, 1800.0, 560.0
+PATIENCE, HELP = 0.3, 0.8
+PLAN = {}
 
 
 def helper_of(core, T, topo):
@@ -71,6 +77,110 @@ def bits(m):
     return bin(m).count("1")
 
 
+def overlap_deps(ops, order, regs, banks):
+    hist, deps = {}, {}
+    for k in order:
+        o, d = ops[k], set()
+        touched = [("r", e) for x in o["r"] for e in regs(x)] + [("w", e) for x in o["w"] for e in regs(x)]
+        for kind, (name, lo, hi) in touched:
+            for k2, kind2, lo2, hi2 in hist.get(name, ()):
+                o2 = ops[k2]
+                same = o2["q"] == o["q"] and o2["sem"] is None and o["sem"] is None
+                if banks and name == "ps" and not same and lo // 512 <= (hi2 - 1) // 512 and lo2 // 512 <= (hi - 1) // 512:
+                    d.add(k2)
+                elif lo < hi2 and lo2 < hi and "w" in (kind, kind2) and not (banks and same and o["q"] == "pe"):
+                    d.add(k2)
+        for kind, (name, lo, hi) in touched:
+            h = hist.setdefault(name, [])
+            if kind == "w":
+                h[:] = [x for x in h if not (lo <= x[2] and x[3] <= hi and (x[0] in d or x[0] == k))]
+            h.append((k, kind, lo, hi))
+        deps[k] = d
+    return deps
+
+
+def plan(ops, deps):
+    n, first = len(ops), {}
+    deps = [set(deps[k]) for k in range(n)]
+    for k, o in enumerate(ops):
+        for u in o["units"]:
+            if first.setdefault(u, k) != k:
+                deps[first[u]] |= {d for d in deps[k] if u not in ops[d]["units"]}
+    after = [[] for _ in range(n)]
+    for k in range(n):
+        for d in deps[k]:
+            after[d].append(k)
+    urgency, seen = [0.0] * n, [False] * n
+
+    def weigh(k):
+        if not seen[k]:
+            seen[k] = True
+            urgency[k] = max([-1000.0 * DUE.get(ops[k]["piece"], 200)] + [weigh(j) + WAKE for j in after[k]]) + ops[k]["hold"] + ops[k]["lat"]
+        return urgency[k]
+    for k in range(n - 1, -1, -1):
+        weigh(k)
+    left = [len(deps[k]) for k in range(n)]
+    ready, took = {"act": {}}, {}
+    for k in range(n):
+        if not left[k]:
+            ready.setdefault(ops[k]["q"], {})[k] = 0.0
+    free, order, ring, ring_free, users, end = {}, [], {}, {b: 0.0 for b in RING}, {}, [0.0] * n
+    for o in ops:
+        for u in o["units"]:
+            users[u] = users.get(u, 0) + 1
+    while len(order) < n:
+        best = None
+        for q, rq in ready.items():
+            cand, fq = [], free.get(q, 0.0)
+            for k, t in rq.items():
+                o = ops[k]
+                if o["units"] and any(u not in ring for u in o["units"]):
+                    if not ring_free:
+                        continue
+                    t = max(t, min(ring_free.values()))
+                for e in o["eng"]:
+                    t = max(t, free.get(e, 0.0))
+                cand.append((max(t, fq), k))
+            if q == "act":
+                mine = min(cand)[0] if cand else 1e9
+                cand += [(max(t, fq), k) for k, t in ready.get("dve", {}).items() if ops[k]["alt"] and max(t, fq) + HELP * ops[k]["hold"] < mine]
+            if not cand:
+                continue
+            t0 = min(cand)[0]
+            k = max((k for t, k in cand if t == t0), key=lambda k: urgency[k])
+            while True:
+                span = PATIENCE * max([ops[k]["hold"]] + list(ops[k]["eng"].values()))
+                soon = [(t, j) for t, j in cand if t < t0 + span and urgency[j] > urgency[k] + span]
+                if not soon:
+                    break
+                t0, k = max(soon, key=lambda x: urgency[x[1]])
+            if best is None or (t0, q == "act") < (best[0], best[2] == "act"):
+                best = (t0, k, q)
+        t0, k, q = best
+        o = ops[k]
+        del ready[o["q"]][k]
+        order.append(k)
+        took[k] = q
+        free[q] = t0 + o["hold"]
+        for e, d in o["eng"].items():
+            free[e] = t0 + d
+        end[k] = t0 + o["hold"] + o["lat"]
+        for u in o["units"]:
+            if u not in ring:
+                ring[u] = min(ring_free, key=lambda b: ring_free[b])
+                del ring_free[ring[u]]
+            users[u] -= 1
+            if not users[u]:
+                ring_free[ring[u]] = end[k] + WAKE
+        for j in after[k]:
+            left[j] -= 1
+            if not left[j]:
+                ready.setdefault(ops[j]["q"], {})[j] = max(end[d] for d in deps[j]) + WAKE
+    order.sort(key=lambda k: (0, k) if ops[k]["sem"] and not deps[k] else (1, 0))
+    PLAN["end"] = end
+    return order, ring, took
+
+
 def rank_program(g, core, T, topo):
     rank = T.rank_of(core)
     if rank is None:
@@ -78,110 +188,154 @@ def rank_program(g, core, T, topo):
             if helper_of(owner, T, topo) == core:
                 rid, pid = topo.addr(owner)[:2]
                 m_out = topo.mask(core, owner)
-                for k in [int(t[4:]) for t in ORDER if t[:4] == "fold"]:
-                    lo, hi = FOLD[k]
+                for k in range(NFOLD):
+                    x = T.R[:, FOLDS[k][4]:FOLDS[k][4] + FOLDS[k][3]]
                     g.wait_ge(T.sem["f%d" % k], bits(fold_mask(k, owner, T, topo)))
-                    g.remote_dma(T.R[:, lo:hi], T.R[:, lo:hi], T.sem["b%d" % k], T.sem.hl, pid, rid, m_out)
+                    g.remote_dma(x, x, T.sem["b%d" % k], T.sem.hl, pid, rid, m_out)
                 g.wait_ge(T.sem.hl, NFOLD * bits(m_out))
         return
     N = len(T.cores)
     nxt, prv, hlp = T.cores[(rank + 1) % N], T.cores[(rank - 1) % N], helper_of(core, T, topo)
-    ops = []
+    ops, ring, tag = [], {}, [None]
 
-    def v(name, lo=None, hi=None, step=1):
+    def v(name, lo=None, hi=None, step=1, rows=None, unit=None):
         if name in LODGE:
             name, lo, hi = LODGE[name][0], LODGE[name][1] + lo, LODGE[name][1] + hi
-        t = T[name]
         if lo is None:
-            lo, hi = 0, t.shape[1]
-        if name == "ps":
-            reg = [("ps", b, b + 1, lo, hi) for b in range(lo // 512, (hi - 1) // 512 + 1)]
-        else:
-            reg = [(name, lo, hi)]
-        return (t[:, lo:hi] if step == 1 else t[:, lo:hi:step], reg)
+            lo, hi = 0, SCRATCH[name][1][1]
+        n = len(range(lo, hi, step)) * (rows[1] - rows[0] if rows else 1)
+        return {"name": name, "lo": lo, "hi": hi, "step": step, "rows": rows, "unit": unit, "off": None, "n": n, "b": BYTES[SCRATCH[name][2]]}
 
     def v3(name, i0, i1, lo, hi):
-        reg = [(name, i * 512 + lo, i * 512 + hi) for i in range(i0, i1)]
-        return (T[name][:, i0, lo:hi] if i1 == i0 + 1 else T[name][:, i0:i1, lo:hi], reg)
+        return v(name, lo, hi, rows=(i0, i1))
 
     def ind(win, off):
-        return (win[0].indirect(off[0]), win[1], off[1])
+        return dict(win, off=off, n=16 * off["n"])
 
-    def op(q, fn, reads, writes, sem=None, inc=1):
-        rr, ww = [], []
-        for x in reads:
-            if isinstance(x, tuple):
-                rr += x[1] + (x[2] if len(x) > 2 else [])
-        for x in writes:
-            ww += x[1]
-            rr += x[2] if len(x) > 2 else []
-        ops.append({"q": q, "fn": fn, "r": rr, "w": ww, "sem": sem, "inc": inc})
+    def hbm(t, n, reg=None):
+        return {"name": None, "ap": t, "off": None, "unit": None, "n": n, "b": 4, "reg": [reg] if reg else []}
 
-    def val(x):
-        return x[0] if isinstance(x, tuple) else x
+    def ap(x):
+        if not isinstance(x, dict):
+            return x
+        if x["name"] is None:
+            return x["ap"]
+        t, b = T[x["name"]], ring[x["unit"]] if x["unit"] is not None else 0
+        if x["rows"]:
+            i0, i1 = x["rows"]
+            return t[:, i0, x["lo"]:x["hi"]] if i1 == i0 + 1 else t[:, i0:i1, x["lo"]:x["hi"]]
+        a = t[:, b + x["lo"]:b + x["hi"]] if x["step"] == 1 else t[:, b + x["lo"]:b + x["hi"]:x["step"]]
+        return a.indirect(ap(x["off"])) if x["off"] else a
 
-    def mm(out, l, r, start, stop):
-        op("pe", lambda: g.tensor.matmul(out[0], l[0], r[0], start, stop), [l, r], [out])
+    def regs(x):
+        if x["name"] is None:
+            return x["reg"]
+        if x["rows"]:
+            return [(x["name"], i * 512 + x["lo"], i * 512 + x["hi"]) for i in range(*x["rows"])]
+        if x["unit"] is None:
+            return [(x["name"], x["lo"], x["hi"])]
+        if ring:
+            return [("ps", ring[x["unit"]] + x["lo"], ring[x["unit"]] + x["hi"])]
+        return [("unit%d" % x["unit"], x["lo"] // 512 * 512, (x["hi"] + 511) // 512 * 512)]
+
+    def op(q, fn, reads, writes, hold, sem=None, inc=1, lat=0.0, join=False, follows=(), eng=None):
+        rr = [x for x in reads if isinstance(x, dict)]
+        rr += [x["off"] for x in rr + writes if x["off"]]
+        units = {x["unit"] for x in rr + writes if x["unit"] is not None}
+        if q in ("pe", "act", "dve"):
+            eng = {"bank%d" % (x["lo"] // 512): hold for x in rr + writes if x["name"] == "ps" and x["unit"] is None}
+        if join:
+            o = ops[-1]
+            o["fn"].append(fn)
+            o["r"] += rr
+            o["w"] += writes
+            o["hold"] += hold
+            o["units"] |= units
+            o["eng"] = {e: o["hold"] for e in list(o["eng"]) + list(eng)}
+        else:
+            ops.append({"q": q, "fn": [fn], "r": rr, "w": list(writes), "sem": sem, "inc": inc, "hold": hold, "lat": lat, "units": units,
+                        "follows": list(follows), "eng": eng or {}, "piece": tag[0], "alt": None})
+        return len(ops) - 1
+
+    def mm(out, l, r, start, stop, join=False):
+        op("pe", lambda: g.tensor.matmul(ap(out), ap(l), ap(r), start, stop), [l, r], [out],
+           max(min(64, l["n"]), r["n"]) * (4 if l["b"] == 4 else 1) * PE_CYCLE, join=join)
+
+    def vec(fn, reads, out, two=False):
+        wide = [x for x in reads + [out] if isinstance(x, dict) and x["n"] == out["n"]]
+        if out["off"] or any(x["off"] for x in wide):
+            hold = CALL + out["n"] * (SCATTER if out["off"] else GATHER)
+        else:
+            hold = CALL + max(64, out["n"] * (0.5 if all(x["b"] == 2 for x in wide) else 1) * (2 if two else 1)) * CYCLE
+        op("dve", fn, reads, [out], hold)
 
     def cp(out, a):
-        op("dve", lambda: g.vector.tensor_copy(out[0], a[0]), [a], [out])
+        vec(lambda: g.vector.tensor_copy(ap(out), ap(a)), [a], out)
 
     def tt(out, a, b, o):
-        op("dve", lambda: g.vector.tensor_tensor(out[0], a[0], b[0], o), [a, b], [out])
+        vec(lambda: g.vector.tensor_tensor(ap(out), ap(a), ap(b), o), [a, b], out, "ps" not in (a["name"], b["name"]))
 
     def ts(out, a, s1, o0, s2=None, o1=None):
         if o1 is None:
-            op("dve", lambda: g.vector.tensor_scalar(out[0], a[0], val(s1), None, o0), [a, s1], [out])
+            vec(lambda: g.vector.tensor_scalar(ap(out), ap(a), ap(s1), None, o0), [a, s1], out)
         else:
-            op("dve", lambda: g.vector.tensor_scalar(out[0], a[0], val(s1), val(s2), o0, o1), [a, s1, s2], [out])
+            vec(lambda: g.vector.tensor_scalar(ap(out), ap(a), ap(s1), ap(s2), o0, o1), [a, s1, s2], out)
+
+    def affine(out, a, scale, bias):
+        ts(out, a, scale, A.mult, bias, A.add)
+        ops[-1]["alt"] = lambda: g.scalar.activation(ap(out), ap(a), AF.Identity, bias=bias, scale=scale)
 
     def scan(out, d0, d1, o0, o1):
-        op("dve", lambda: g.vector.tensor_tensor_scan(out[0], d0[0], d1[0], 0.0, o0, o1), [d0, d1], [out])
+        vec(lambda: g.vector.tensor_tensor_scan(ap(out), ap(d0), ap(d1), 0.0, o0, o1), [d0, d1], out)
 
     def turn(out, a):
-        op("dve", lambda: g.vector.transpose(out[0], a[0]), [a], [out])
+        vec(lambda: g.vector.transpose(ap(out), ap(a)), [a], out)
 
     def fill(out, c):
-        op("dve", lambda: g.vector.memset(out[0], c), [], [out])
+        vec(lambda: g.vector.memset(ap(out), c), [], out)
 
     def act(out, a, f, bias=0.0, scale=1.0):
-        op("act", lambda: g.scalar.activation(out[0], a[0], f, bias=val(bias), scale=val(scale)), [a, bias, scale], [out])
+        op("act", lambda: g.scalar.activation(ap(out), ap(a), f, bias=ap(bias), scale=ap(scale)), [a, bias, scale], [out], 2 * CALL + out["n"] * CYCLE)
 
-    def iota(out, pat, base, cm, flt):
-        if flt:
-            op("pool", lambda: g.iota(out[0], pat, base, cm, allow_small_or_imprecise_dtypes=True), [], [out])
+    def iota(out, pat, base, cm):
+        if SCRATCH[out["name"]][2] == "int32":
+            op("pool", lambda: g.iota(ap(out), pat, base, cm), [], [out], 130 + 2 * out["n"] * CYCLE)
         else:
-            op("pool", lambda: g.iota(out[0], pat, base, cm), [], [out])
+            op("pool", lambda: g.iota(ap(out), pat, base, cm, allow_small_or_imprecise_dtypes=True), [], [out], 130 + 2 * out["n"] * CYCLE)
 
-    def sel(out, a, pat, cmp, fl):
-        op("pool", lambda: g.affine_select(out[0], a[0], pat, cmp, fl, 0, 1), [a], [out])
+    def sel(out, pat, cmp, fl, base=0):
+        op("pool", lambda: g.affine_select(ap(out), ap(out), pat, cmp, fl, base, 1), [out], [out], 170 + 2 * out["n"] * CYCLE)
 
-    nd, nl = [0], [0]
+    nd, nl, last = [0], [0], {}
 
-    def dma(q, out, a):
+    def dma(q, out, a, behind=0):
         e = g.sync if q == "sp" else g.scalar
-        op(q, lambda: e.dma_start(out[0], a[0]), [a], [out], sem="d%d" % nd[0], inc=16)
+        op(q, lambda: e.dma_start(ap(out), ap(a)), [a], [out], 0, sem="d%d" % nd[0], inc=16,
+           lat=DMA_FIX + 128 * (out["n"] * out["b"] + behind) / DMA_RATE)
         nd[0] += 1
-
-    def hbm(t):
-        return (t, [])
 
     def send(k, out, a):
         rid, pid = topo.addr(nxt)[:2]
         mk, ls = topo.mask(core, nxt), "l%d" % nl[0]
         nl[0] += 1
-        op("pool", lambda: g.remote_dma(out[0], a[0], T.sem["a%d" % k], T.sem[ls], pid, rid, mk), [a], [], sem=ls, inc=-bits(mk))
-        op("far", None, [], [out], sem="a%d" % k, inc=bits(topo.mask(prv, core)))
+        j = op("pool", lambda: g.remote_dma(ap(out), ap(a), T.sem["a%d" % k], T.sem[ls], pid, rid, mk), [a], [], 300, sem=ls, inc=-bits(mk),
+               lat=1.5 * DMA_FIX, eng={"out": DMA_FIX / 2})
+        last[k] = j
+        op("far", None, [], [out], 0, sem="a%d" % k, inc=bits(topo.mask(prv, core)), lat=DMA_FIX / 2, follows=[j])
 
-    def fold(k, srcs):
+    def fold(k):
         rid, pid = topo.addr(hlp)[:2]
         mk, ls = fold_mask(k, core, T, topo), "l%d" % nl[0]
         nl[0] += 1
-        out = v("R", *FOLD[k])
-        op("pool", lambda: g.remote_dma_fused([RemoteDMATransfer(
+        an, slots, lo, n, c = FOLDS[k]
+        out, srcs = v("R", c, c + n), [v3(an, i, i + 1, lo, lo + n) for i in slots]
+        used = [out] if c in [x[4] for x in FOLDS[:k]] else []
+        span = 128 * len(srcs) * (4 * n + 600) / DMA_RATE * (2 if k in NARROW else 1)
+        last["fold"] = op("pool", lambda: g.remote_dma_fused([RemoteDMATransfer(
             dst_ids=[DstId(rid=rid, pnc=pid)], dma_engine_mask=mk, remote_sem=T.sem["f%d" % k],
-            srcs=[s[0] for s in srcs], dsts=[out[0]], alu_op=1)], local_sem=T.sem[ls]), srcs, [], sem=ls, inc=-bits(mk))
-        op("far", None, [], [out], sem="b%d" % k, inc=bits(topo.mask(hlp, core)))
+            srcs=[ap(s) for s in srcs], dsts=[ap(out)], alu_op=1)], local_sem=T.sem[ls]), srcs, used, 300, sem=ls, inc=-bits(mk),
+            lat=DMA_FIX + span, follows=[last[x] for x in ("fold",) + BEHIND.get(k, ()) if x in last], eng={"in": span} if k in NARROW else {"in": span, "out": span})
+        op("far", None, [], [out], 0, sem="b%d" % k, inc=bits(topo.mask(hlp, core)), lat=1.5 * DMA_FIX, follows=[last["fold"]])
 
     LEVEL = [0, 0, 1, 0, 0, 1]
     TIMES = [[0], [1], [0, 1], [2], [3], [2, 3]]
@@ -189,18 +343,17 @@ def rank_program(g, core, T, topo):
     RCU = [2, 3, 8, 5, 6, 9]
     NWIN = [n0(0), n0(1), n0(0), n0(2), n0(4), n0(3)]
     XWIN = [n0(0), n0(0), n0(0), n0(2), n0(2), n0(0)]
-    PG = {"c0": "Pg0", "c2": "Pg1", "c1": "Pg2", "c3": "Pg0", "c4": "Pg1", "c5": "Pg2", "r2": "Pg0", "r4": "Pg1", "r5": "Pg2",
-          "r0": "Pg2", "r1": "Pg0", "r3": "Pg1"}
     AB = {"c0": ("A0", 0), "c2": ("A0", S), "c1": ("A1", 0), "c3": ("A1", S), "r0": ("A2", 0), "r1": ("A2", S),
           "c5": ("A3", 0), "c4": ("A3", S), "r2": ("A0", 0), "r3": ("A0", S), "r4": ("A1", 0), "r5": ("A1", S)}
-    I1, IH, IQ, IE = (v("Ib", k * 128, k * 128 + 128) for k in range(4))
+    SCALES = (1.0, 0.5, -0.25, -0.125, -1.0, -2.0)
+    I1, IH, IQ, IE, IN, I2 = (v("Ib", k * 128, k * 128 + 128) for k in range(6))
     qf = v("cfl", 0, 1)
-    dbuf = [0]
-    KEY, XQ, EL, TW = [2048, 3584], [2560, 2816], [3072, 3088], 3328
+    nu = [0]
 
-    def ring():
-        dbuf[0] ^= 1
-        return dbuf[0] * 1024
+    def buf():
+        nu[0] += 1
+        u = nu[0]
+        return lambda lo, hi, step=1: v("ps", lo, hi, step, unit=u)
 
     def cut(k, lo=0, hi=S):
         return v("cu", k * S + lo, k * S + hi)
@@ -208,32 +361,34 @@ def rank_program(g, core, T, topo):
     def ob(kind, k):
         return v("ob" + kind, k * 16, k * 16 + 16)
 
-    def cand_f(m, lo, hi):
-        if m in (0, 2, 5):
-            k = {0: 0, 2: 1, 5: 2}[m]
-            return v("cf", k * S + lo, k * S + hi)
-        b = n0({1: 0, 3: 1, 4: 3}[m])
-        return v("U", b + lo, b + hi)
+    def succ(lo, hi):
+        return v("U", OFF + lo, OFF + hi)
+
+    def sym(t, lo=0, hi=S):
+        return v("nx", t // 2 * 2 * S + 2 * lo + t % 2, t // 2 * 2 * S + 2 * hi, 2)
+
+    def do(piece, fn, *a):
+        tag[0] = piece
+        fn(*a)
 
     def load():
-        dma("sp", v("str"), hbm(T.st[:]))
-        dma("act", v("sur", OFF, OFF + F), hbm(T.su[:]))
-        dma("sp", v("P", OFF, OFF + F), hbm(T.th[:]))
-        dma("sp", v("xa", 0, 512), hbm(T.xs[:, 0:512]))
-        dma("act", v("hvr"), hbm(T.hv[:]))
-        dma("sp", v("xb", 0, 512), hbm(T.xs[:, 512:1024]))
+        dma("act", v("hvr"), hbm(T.hv[:], 16))
+        dma("sp", v("str"), hbm(T.st[:], 32))
+        dma("act", succ(0, F), hbm(T.su[:], F))
+        dma("sp", v("P", 0, F), hbm(T.th[:], F), 4 * F)
+        dma("act", v("xa", 0, 2 * S), hbm(T.xs[:, 0:2 * S], 2 * S), 8 * F)
+        dma("sp", v("xb", 0, 2 * S), hbm(T.xs[:, 2 * S:4 * S], 2 * S), 8 * F + 8 * S)
         fill(v("I32"), 1.0)
-        fill(v("Dm"), -1.0)
-        fill(v("P", 0, OFF), 0)
-        fill(v("sur", 0, OFF), 0)
-        fill(v("U", 0, OFF), 0.0)
-        iota(v("ci", 0, 1), [[0, 1]], 0, 1, False)
-        iota(v("jr"), [[0, 16], [1, 16]], 0, 0, True)
-        sel(v("I32"), v("I32"), [[-1, 128]], A.is_equal, 0.0)
-        iota(v("ci", 16, 32), [[16, 16]], 15, 0, False)
-        iota(v("Nm"), [[1, 6 * S]], n0(0), 0, True)
-        sel(v("Dm"), v("Dm"), [[0, 15], [-16, 8], [-1, 16]], A.is_equal, 0.0)
-        sel(v("Dm"), v("Dm"), [[-1, 15], [-16, 8], [0, 16]], A.not_equal, 1.0)
+        fill(v("Jb"), 1.0)
+        fill(v("c2k"), 2048.0)
+        fill(v("U", 0, OFF), 0)
+        iota(v("ci", 0, 1), [[0, 1]], 0, 1)
+        iota(v("jr"), [[0, 16], [1, 16]], 0, 0)
+        sel(v("I32"), [[-1, 128]], A.is_equal, 0.0)
+        sel(v("Jb"), [[-16, 8], [1, 16]], A.is_equal, 0.0, -15)
+        iota(v("ci", 16, 32), [[16, 16]], 15, 0)
+        iota(v("e1"), [[1, S]], n0(0), 0)
+        iota(v("e2", 0, 128), [[1, 8], [0, 16]], 0, 0)
         ts(v("ci", 1, 2), v("ci", 0, 1), 15, A.bitwise_and)
         ts(v("ci", 2, 3), v("ci", 0, 1), 4, A.logical_shift_right)
         ts(v("big"), v("jr"), 0.0, A.is_equal, 2.0 ** 40, A.mult)
@@ -247,289 +402,280 @@ def rank_program(g, core, T, topo):
         for k, c in enumerate((3.0, 4.0, 260.0)):
             ts(v("rdo", k, k + 1), v("cfl", 2, 3), 16.0, A.mult, c, A.add)
         ts(v("blk", 0, 8), v("jr", 0, 8), v("cfl", 1, 2), A.is_equal)
-        ts(v("blk", 8, 16), v("jr", 0, 8), v("cfl", 1, 2), A.is_equal, 2.0 ** 17, A.mult)
+        ts(v("blk", 8, 16), v("jr", 0, 8), v("cfl", 1, 2), A.is_equal, 2.0 ** 13, A.mult)
         cp(v("bco"), v("ci", 16, 32))
-        ts(v("obu", 0, 32), v("str"), float(OFF), A.add)
-        ts(v("obf", 0, 32), v("str"), float(OFF), A.add)
-        ts(v("obh", 0, 32), v("str"), float(OFF - 2048), A.add, 2.0 ** -6, A.mult)
-        for k, c in enumerate((1.0, 0.5, -0.25, -0.125)):
+        ts(v("cfl", 3, 4), qf, float(S), A.mult)
+        ts(v("e1"), v("e1"), v("cfl", 3, 4), A.add)
+        ts(v("e2", 0, 128), v("e2", 0, 128), v("cfl", 1, 2), A.is_equal)
+        tt(v("xd"), v("e2", 0, 128), v("I32"), A.add)
+        ts(v("e4", 0, 16), v("dl", 0, 16), -1.0, A.mult, 2.0, A.add)
+        ts(v("e4", 16, 32), v("dl", 0, 16), -2.0 / 64, A.mult, 1.0 / 64, A.add)
+        for j in range(15):
+            ts(v("Dm", j * 128, j * 128 + 128), v("xd"), v("e4", j, j + 1), A.is_equal, v("e4", 16 + j, 17 + j), A.mult)
+        cp(v("obu", 0, 32), v("str"))
+        ts(v("obh", 0, 32), v("str"), -2048.0, A.add)
+        for k, c in enumerate(SCALES):
             act(v("Ib", k * 128, k * 128 + 128), v("I32"), AF.Copy, scale=c)
-        act(v("slr"), v("jr"), AF.Copy, scale=4096.0)
-        act(v("lnh"), v("hvr"), AF.Ln, scale=1.0 / 16)
+        tt(v("hf"), v("Ib", 128, 256, 2), v("Ib", 129, 256, 2), A.add)
         for m in range(6):
-            act(v("Nm", m * S, m * S + S), v("Nm", m * S, m * S + S), AF.Copy, scale=v("dl", m, m + 1))
+            act(v("Nm", m * S, m * S + S), v("e1"), AF.Copy, scale=v("dl", m, m + 1))
+        tag[0] = "ln"
+        y, e = v("lnh", 16, 32), v("lnh", 32, 48)
+        ts(y, v("hvr"), 0.9, A.mult, -1.05, A.add)
+        for k in range(4):
+            act(e, y, AF.Exp, bias=float(k), scale=-1.0)
+            tt(e, e, v("hvr"), A.mult)
+            tt(y, y, e, A.add)
+        ts(v("lnh", 0, 16), y, -4.0 - math.log(16.0), A.add)
+        tag[0] = "load"
+        for k in range(2):
+            cp(cut(k), ind(succ(0, F), ob("u", k)))
+        for t in range(4):
+            affine(sym(t), v("xb" if t > 1 else "xa", t % 2 * S, t % 2 * S + S), -1.0, 2048.0)
 
-    def first(k):
-        ts(cut(k), ind(v("sur"), ob("u", k)), float(OFF), A.add)
-
-    def conv_u(lo, hi):
-        ts(v("U", lo, hi), v("sur", lo, hi), float(OFF), A.add)
-
-    def conv_x(k):
-        ts(v("nx", k * 512, k * 512 + 512), v("xb" if k else "xa", 0, 512), -1.0, A.mult, 2048.0, A.add)
-
-    def neg_p(m):
-        ts(v("nP", m * S, m * S + S), v("P", n0(m), n0(m) + S), -1.0, A.mult, 2048.0, A.add)
-
-    def gather(name, q, quarters=1, parts=1):
-        m, n = int(name[1]), int(64 * quarters) // parts
+    def gather(name):
+        m, n = int(name[1]), S // CUT[name]
         k, w = (CAND[m], NWIN[m]) if name[0] == "c" else (RCU[m], n0(m + 1))
-        for s in range(int(q * 64), int((q + quarters) * 64), n):
-            ts(v(PG[name], s * 16, (s + n) * 16), ind(v("P", 0, w), cut(k, s, s + n)), -2048.0, A.add)
+        for s in range(0, S, n):
+            affine(v(PG[name], s * 16, (s + n) * 16), ind(v("P", 0, w), cut(k, s, s + n)), 1.0, -2048.0)
 
-    def prep(m):
-        kb, tm = KEY[LEVEL[m]], TIMES[m]
+    def unit(name, s0, s1, i0, i1):
+        m, b, n = int(name[1]), buf(), s1 - s0
+        for i in range(i0, i1):
+            o = b((i - i0) * n, (i - i0 + 1) * n)
+            mm(o, I1, v(PG[name], s0 * 16 + i, s1 * 16, 16), True, False, join=(i - i0) * n % 512 > 0)
+            if name[0] == "r":
+                mm(o, I1, v("nP", m * S + s0, m * S + s1), False, True, join=True)
+            elif LEVEL[m]:
+                mm(o, v("xt%d" % m, 2 * s0, 2 * s1), v("hf"), False, True, join=True)
+            else:
+                mm(o, I1, sym(TIMES[m][0], s0, s1), False, True, join=True)
+        an, ao = AB[name]
+        act(v3(an, i0, i1, ao + s0, ao + s1), b(0, (i1 - i0) * n), AF.Abs)
+
+    def scores(m):
+        name, kb, lv = "c%d" % m, KEY[LEVEL[m]], LEVEL[m]
+        an, ao = AB[name]
+        do("g%d" % m, gather, name)
+        tag[0] = "sc%d" % m
+        ts(v("ch", lv * S, lv * S + S), cut(CAND[m]), -2048.0, A.add)
+        mm(v("ps", kb + S, kb + 2 * S), I1, v("c2k"), True, False)
         for h in range(2):
-            mm(v("ps", kb + S + h * 128, kb + S + h * 128 + 128), cand_f(m, h * 128, h * 128 + 128), v("I32"), True, True)
-        for k, t in enumerate(tm):
-            mm(v("ps", XQ[LEVEL[m]], XQ[LEVEL[m]] + S), IQ if len(tm) == 1 else IE, v("nx", t * S, t * S + S), k == 0, k == len(tm) - 1)
-        mm(v("ps", kb, kb + S), I1, v("slr"), True, False)
+            mm(v("ps", kb + S + h * 128, kb + S + h * 128 + 128), v("ch", lv * S + h * 128, lv * S + h * 128 + 128), v("Jb"), False, h == 1, join=True)
+        if lv:
+            b, t = buf(), TIMES[m][0]
+            for q in range(4):
+                mm(b(q * 128, q * 128 + 128), v("nx", t * S + q * 128, t * S + q * 128 + 128), I1, True, True, join=q > 0)
+            act(v("xt%d" % m, 0, 512), b(0, 512), AF.Copy)
+        for h in range(2):
+            quarters = lv or (m == 0 and h == 0)
+            if quarters:
+                unit(name, h * 128, h * 128 + 64, 0, 16), unit(name, h * 128 + 64, h * 128 + 128, 0, 16)
+            for i0 in (0, 8):
+                if not quarters:
+                    unit(name, h * 128, h * 128 + 128, i0, i0 + 8)
+                for i in range(i0, i0 + 8):
+                    mm(v("ps", kb + h * 128 + 15 - i, kb + h * 128 + 128, 16), v3(an, i, i + 1, ao + h * 128, ao + h * 128 + 128), v("blk", 8, 16),
+                       True, True, join=i % 4 > 0)
 
-    def unit(name, u):
-        m, h, b = int(name[1]), u // 2, ring()
-        subs = [("nx", t) for t in TIMES[m]] if name[0] == "c" else [("nP", m)]
-        for j in range(8):
-            o = v("ps", b + j * 128, b + j * 128 + 128)
-            mm(o, I1, v(PG[name], h * 2048 + (u % 2) * 8 + j, h * 2048 + 2048, 16), True, False)
-            for k, (t, c) in enumerate(subs):
-                mm(o, I1 if len(subs) == 1 else IH, v(t, c * S + h * 128, c * S + h * 128 + 128), False, k == len(subs) - 1)
-        an, ao = AB[name]
-        x = v3(an, (u % 2) * 8, (u % 2) * 8 + 8, ao + h * 128, ao + h * 128 + 128)
-        if "%su%d" % (name, u) in ON_VECTOR:
-            ts(x, v("ps", b, b + 1024), -1.0, A.mult)
-            tt(x, v("ps", b, b + 1024), x, A.max)
-        else:
-            act(x, v("ps", b, b + 1024), AF.Abs)
-
-    def score(m, u):
+    def exp_c(m):
         an, ao = AB["c%d" % m]
-        h, kb = u // 2, KEY[LEVEL[m]]
-        for j in range(8):
-            i = (u % 2) * 8 + j
-            mm(v("ps", kb + h * 128 + i, kb + h * 128 + 128, 16), v3(an, i, i + 1, ao + h * 128, ao + h * 128 + 128), v("blk", 8, 16),
-               False, u == 3 and j == 7)
+        n = 16 // EXP_CALLS
+        for i in range(0, 16, n):
+            x = v3(an, i, i + n, ao, ao + S)
+            act(x, x, AF.Exp, bias=-math.log(16.0 * (1 + LEVEL[m])), scale=-1.0 / 512)
 
-    def exp_c(m, u):
-        an, ao = AB["c%d" % m]
-        x = v3(an, (u % 2) * 8, (u % 2) * 8 + 8, ao + (u // 2) * 128, ao + (u // 2) * 128 + 128)
-        act(x, x, AF.Exp, bias=-math.log(16.0 * (1 + LEVEL[m])), scale=-1.0 / 512)
+    def by_max(m):
+        return [i for ms, (lo, hi) in BY_MAX.items() if m in ms for i in range(lo, hi)]
 
-    def unit_r(m, slots):
-        name, b = "r%d" % m, ring()
-        for j, i in enumerate(slots):
-            o = v("ps", b + j * S, b + j * S + S)
-            mm(o, I1, v(PG[name], i, 4096, 16), True, False)
-            mm(o, I1, v("nP", m * S, m * S + S), False, True)
-        an, ao = AB[name]
-        act(v3(an, slots[0], slots[-1] + 1, ao, ao + S), v("ps", b, b + len(slots) * S), AF.Abs)
+    def sizes(m, skip=()):
+        name = "r%d" % m
+        tag[0] = "size%d" % m
+        affine(v("nP", m * S, m * S + S), v("P", n0(m), n0(m) + S), -1.0, 2048.0)
+        slots = [i for i in range(16) if i not in skip and i not in by_max(m)]
+        if name in CUT:
+            do("rg%d" % m, gather, name)
+            tag[0] = "size%d" % m
+            for h in range(2):
+                for j in range(0, len(slots), 8):
+                    unit(name, h * 128, h * 128 + 128, slots[j], slots[j:j + 8][-1] + 1)
+            return
+        run = []
+        for i in range(17):
+            if run and (i not in slots or len(run) == 4):
+                unit(name, 0, S, run[0], run[-1] + 1)
+                run = []
+            if i in slots:
+                run.append(i)
 
-    def exp_r(an, slots, lo, hi):
+    def maxima(ms):
+        lo, hi = BY_MAX[ms]
+        w = len(ms) * S
+        for j, m in enumerate(ms):
+            tag[0] = "max%d" % m
+            x = buf()(0, S)
+            mm(x, IN, v("nP", m * S, m * S + S), True, True)
+            for i in range(lo, hi):
+                tt(v("mx", (i - lo) * w + j * S, (i - lo) * w + j * S + S), v(PG["r%d" % m], i, 4096, 16), x, A.max)
+        tag[0] = "mexp%d" % ms[0]
+        for i0 in range(lo, hi, 1024 // w):
+            b = buf()
+            for i in range(i0, min(hi, i0 + 1024 // w)):
+                o = (i - i0) * w
+                mm(b(o, o + w), I2, v("mx", (i - lo) * w, (i - lo + 1) * w), True, False, join=o % 512 > 0)
+                mm(b(o, o + w), IN, v("nP", ms[0] * S, ms[0] * S + w), False, False, join=True)
+                for j, m in enumerate(ms):
+                    mm(b(o + j * S, o + j * S + S), I1, v(PG["r%d" % m], i, 4096, 16), False, j == len(ms) - 1, join=True)
+            an, ao = AB["r%d" % ms[0]]
+            for i in range(i0, min(hi, i0 + 1024 // w)):
+                act(v3(an, i, i + 1, ao, ao + w), b((i - i0) * w, (i - i0 + 1) * w), AF.Exp, bias=v("lnh", i, i + 1), scale=1.0 / 512)
+
+    def by_maxima(ma, mb):
+        for ms in BY_MAX:
+            if ms[0] in (ma, mb):
+                maxima(ms)
+
+    def exp_r(ma, mb, slots):
         for i in slots:
-            x = v3(an, i, i + 1, lo, hi)
-            act(x, x, AF.Exp, bias=v("lnh", i, i + 1), scale=-1.0 / 512)
+            ms = [m for m in (ma, mb) if i not in by_max(m)]
+            if ms:
+                an, ao = AB["r%d" % ms[0]]
+                x = v3(an, i, i + 1, ao, ao + len(ms) * S)
+                act(x, x, AF.Exp, bias=v("lnh", i, i + 1), scale=-1.0 / 512)
 
     def elect(m):
-        kb, el = KEY[LEVEL[m]], EL[LEVEL[m]]
-        key = v("ps", kb, kb + S)
+        tag[0] = "el%d" % m
+        kb, tm = KEY[LEVEL[m]], TIMES[m]
+        key, low = v("ps", kb, kb + S), v("ps", kb + S, kb + 2 * S)
         scan(v("e1"), v("big"), key, A.add, A.min)
         tt(v("e2"), key, v("e1"), A.subtract)
-        tt(v("e3"), v("ps", kb + S, kb + 2 * S), v("e2"), A.subtract)
+        tt(v("e3"), low, v("e2"), A.subtract)
+        for k, t in enumerate(tm):
+            mm(low, IQ if len(tm) == 1 else IE, sym(t), k == 0, k == len(tm) - 1, join=k > 0)
         scan(v("e4"), v("e2"), v("e3"), A.min, A.max)
         tt(v("e5"), ind(v("e4"), v("bco")), v("dl"), A.mult)
         for h in range(2):
-            mm(v("ps", el + h * 8, el + h * 8 + 8), v("e5", h * 128, h * 128 + 128), v("blk", 0, 8), True, True)
-
-    def won(m):
-        cp(ob("u", 2 + m), v("ps", EL[LEVEL[m]], EL[LEVEL[m]] + 16))
-
-    def keep(m):
-        ts(ob("h", 2 + m), ob("u", 2 + m), -2048.0, A.add, 2.0 ** -6, A.mult)
-
-    def snap(m):
-        ts(v("t1", 0, S), ind(v("P", 0, NWIN[m]), ob("u", 2 + m)), 0.75, A.mult, 512.0 - (0.375 if LEVEL[m] == 0 else 0.4375), A.add)
+            mm(v("ps", kb + h * 8, kb + h * 8 + 8), v("e5", h * 128, h * 128 + 128), v("blk", 0, 8), True, True, join=h > 0)
+        cp(ob("u", 2 + m), v("ps", kb, kb + 16))
+        if m < 4:
+            ts(ob("h", 2 + m), ob("u", 2 + m), -2048.0, A.add)
+        affine(v("t1", 0, S), ind(v("P", 0, NWIN[m]), ob("u", 2 + m)), 0.75, 512.0 - (0.375 if LEVEL[m] == 0 else 0.4375))
         out = v("P", n0(m), n0(m) + S) if LEVEL[m] == 0 else v("sn", (m // 3) * S, (m // 3) * S + S)
-        tt(out, v("ps", XQ[LEVEL[m]], XQ[LEVEL[m]] + S), v("t1", 0, S), A.add)
+        tt(out, low, v("t1", 0, S), A.add)
+        if LEVEL[m]:
+            send(m // 3 * 2, v("P", n0(m), n0(m + 1)), out)
 
     def column(m):
-        cp(cut(2 + m), ind(v("U", 0, NWIN[m]), ob("u", 2 + m)))
-
-    def place(m):
-        cp(v("U", n0(m), n0(m) + S) if LEVEL[m] == 0 else v("cf", 2 * S, 3 * S), cut(2 + m))
-
-    def twins(m):
-        mm(v("ps", TW, TW + S), I1, v("dmk"), True, False)
-        for j in range(15):
-            mm(v("ps", TW + j + 1, TW + S, 16), v("Dm", j * 128, j * 128 + 128), ob("h", CAND[m]), False, j == 14)
+        tag[0] = "col%d" % m
+        cp(cut(2 + m), ind(succ(0, NWIN[m]), ob("u", 2 + m)))
+        if LEVEL[m]:
+            send(m // 3 * 2 + 1, cut(RCU[m]), cut(2 + m))
+        if m < 4:
+            x, y = succ(n0(m), n0(m + 1)), cut(RCU[m])
+            op("pool", lambda: g.affine_select(ap(x), ap(y), [[0, S]], A.is_equal, 0.0, 0, 0), [y], [x], 170 + 2 * S * CYCLE)
 
     def extend(m):
-        scan(v("pr", 0, S), v("ps", TW, TW + S), v("one"), A.mult, A.add)
-        if m in (0, 1, 4):
-            src = [cand_f(m, c * 16, c * 16 + 16) for c in range(16)]
-        else:
-            cp(v("ua"), ind(v("U", 0, XWIN[m]), ob("u", CAND[m])))
-            src = [v("ua", c * 16, c * 16 + 16) for c in range(16)]
-        ts(v("sm", 0, 16), v("pr", 15, S, 16), 0.0, A.not_equal)
-        el = EL[LEVEL[m]]
-        tt(v("sm", 16, 32), ob("f", CAND[m]) if CAND[m] < 2 else v("ps", el, el + 16), v("sm", 0, 16), A.mult)
-        ts(v("so", 0, 32, 2), v("sm", 16, 32), qf, A.max)
+        tag[0] = "ext%d" % m
+        tw = buf()
+        mm(tw(0, S), I1, v("dmk"), True, False)
+        for j in range(15):
+            mm(tw(j + 1, S, 16), v("Dm", j * 128, j * 128 + 128), ob("h", CAND[m]), False, j == 14, join=True)
+        scan(v("pr", 0, S), tw(0, S), v("one"), A.mult, A.add)
+        tt(v("ua"), ind(succ(0, XWIN[m]), ob("u", CAND[m])), v("Nm", m * S, m * S + S), A.max)
+        ts(v("sm", 0, 16), v("pr", 15, S, 16), 0.0, A.is_equal, -8192.0, A.mult)
+        tt(v("sm", 16, 32), ob("h", CAND[m]), v("sm", 0, 16), A.add)
+        ts(v("so", 0, 32, 2), v("sm", 16, 32), 2048.0 + OFF, A.add, qf, A.max)
         for c in range(15, -1, -1):
-            tt(ind(v("U", 0, XWIN[m]), v("so", 2 * c, 2 * c + 1)), src[c], v("Nm", m * S + c * 16, m * S + c * 16 + 16), A.max)
-
-    def again_lists():
-        b = n0(0)
-        turn(v("TT", 0, 512), v("U", b, b + 512))
-        turn(v("TT", 512, 1056), v("U", b - 16, b + 528))
-        cp(v("ru"), ind(v("TT", 0, 1056), v("rdo", 0, 3)))
+            cp(ind(v("U", 0, OFF + XWIN[m]), v("so", 2 * c, 2 * c + 1)), v("ua", c * 16, c * 16 + 16))
 
     def again():
-        b = ring()
+        turn(v("TT", 0, 512), succ(n0(0), n0(2)))
+        turn(v("TT", 512, 1056), succ(n0(0) - 16, n0(2) + 16))
+        cp(v("ru"), ind(v("TT", 0, 1056), v("rdo", 0, 3)))
+        affine(v("Pr"), ind(v("P", 0, n0(5)), v("ru")), 1.0, -2048.0)
+        b = buf()
         for j, m in enumerate((0, 0, 1)):
-            o = v("ps", b + j * S, b + j * S + S)
-            mm(o, I1, v("Pr", j * S, j * S + S), True, False)
-            mm(o, I1, v("nP", m * S, m * S + S), False, True)
-        act(v3("A2", 3, 4, 0, S), v("ps", b, b + S), AF.Abs)
-        act(v3("A2", 4, 5, 0, 2 * S), v("ps", b + S, b + 3 * S), AF.Abs)
-        x = v3("A2", 3, 4, 0, S)
-        act(x, x, AF.Exp, bias=v("lnh", 3, 4), scale=-1.0 / 512)
-        exp_r("A2", [4], 0, 2 * S)
+            o = b(j * S, j * S + S)
+            mm(o, I1, v("Pr", j * S, j * S + S), True, False, join=j > 0)
+            mm(o, I1, v("nP", m * S, m * S + S), False, True, join=True)
+        act(v3("A2", 3, 4, 0, S), b(0, S), AF.Abs)
+        act(v3("A2", 4, 5, 0, 2 * S), b(S, 3 * S), AF.Abs)
+        exp_r(0, 1, (3, 4))
+        b = buf()(0, 512)
+        for i in (3, 4):
+            mm(b, v("I32"), v3("A2", i, i + 1, 0, 512), i == 3, i == 4)
+        tt(v("R", 1024, 1536), b, v("R", 1024, 1536), A.add)
+
+    def out(t, m, c, n=1, q="sp"):
+        tag[0] = "out"
+        dma(q, hbm(t[:, m * S:(m + n) * S], n * S, (t.name, m, m + n)), v("R", c, c + n * S))
 
     def upper(m, a, b, q):
-        p = ring()
-        x, o = v("ps", p, p + S), 3584 + (m // 3) * S
-        act(x, v("R", a, a + S), AF.Copy, scale=0.5)
+        x, o = buf()(0, S), 2560 + (m // 3) * S
+        ts(x, v("R", a, a + S), 0.5, A.mult)
         tt(x, x, v("R", b, b + S), A.mult)
         tt(v("R", o, o + S), x, v("R", q, q + S), A.add)
-        dma("sp", hbm(T.ym[:, m * S:m * S + S]), v("R", o, o + S))
+        out(T.ym, m, o)
 
-    def out(t, m, c, n=1):
-        dma("sp", hbm(t[:, m * S:(m + n) * S]), v("R", c, c + n * S))
-
-    def slots(an, lo, hi, skip=()):
-        return [v3(an, i, i + 1, lo, hi) for i in range(16) if i not in skip]
-
-    def sum_t(m, k):
-        an, ao = AB["r%d" % m]
-        for i in range(4 * k, 4 * k + 4):
-            exp_r(an, [i], ao, ao + S)
-            mm(v("ps", KEY[0], KEY[0] + S), v("I32"), v3(an, i, i + 1, ao, ao + S), i == 0, i == 15)
-
-    def out_t(m, c):
-        cp(v("R", c, c + S), v("ps", KEY[0], KEY[0] + S))
-        out(T.yz, m, c)
-
-    def out01():
-        b = ring()
-        for k, x in enumerate([v("R", *FOLD[3])] + [v3("A2", i, i + 1, 0, 512) for i in (3, 4)]):
-            mm(v("ps", b, b + 512), v("I32"), x, k == 0, k == 2)
-        cp(v("R", 2560, 3072), v("ps", b, b + 512))
-        out(T.yz, 0, 2560, 2)
-
-    def last(k):
-        for i in range(4 * k, 4 * k + 4):
-            x, acc = v3("A1", i, i + 1, S, 2 * S), v("ps", KEY[1], KEY[1] + S)
-            exp_r("A1", [i], S, 2 * S)
-            if i % 2 == 0:
-                mm(v("ps", XQ[0], XQ[0] + S), v("I32"), x, i == 0, i == 14)
-            elif i == 1:
+    def tail():
+        slots = sorted(range(16), key=lambda i: i in by_max(4))
+        on_pe = [slots[k] for k in TAIL_PE]
+        on_v = [i for i in slots if i not in on_pe]
+        acc, sums, res = v("ps", KEY[1], KEY[1] + 512), v("ps", KEY[0], KEY[0] + 512), v("R", 3072, 3584)
+        exp_r(4, 5, slots)
+        for i in slots:
+            x = v3("A1", i, i + 1, 0, 512)
+            if i in on_pe:
+                mm(sums, v("I32"), x, i == on_pe[0], i == on_pe[-1])
+            elif i == on_v[0]:
                 cp(acc, x)
             else:
-                tt(acc if i < 15 else v("e1"), acc, x, A.add)
-        if k == 3:
-            tt(v("R", 3328, 3584), v("ps", XQ[0], XQ[0] + S), v("e1"), A.add)
-            dma("act", hbm(T.yz[:, 5 * S:6 * S]), v("R", 3328, 3584))
+                tt(acc if i != on_v[-1] else res, acc, x, A.add)
+        tt(res, sums, res, A.add)
+        out(T.yz, 4, 3072, 2, "act")
 
-    Q4 = [[0, 1, 2, 3], [4, 5, 6, 7], [8, 9, 10, 11], [12, 13, 14, 15]]
-    Q0 = [[0, 1, 2], [5, 6, 7, 8], [9, 10, 11, 12], [13, 14, 15]]
-    Q1 = [[0, 1, 2, 3]] + Q0[1:]
-    piece = {"load": (load,), "u0": (conv_u, OFF, 1008), "u1": (conv_u, 1008, OFF + F), "x0": (conv_x, 0), "x1": (conv_x, 1),
-             "lists": (again_lists,), "gagain": (ts, v("Pr", 0, 768), ind(v("P", 0, n0(5)), v("ru")), -2048.0, A.add), "again": (again,),
-             "send0": (send, 0, v("P", n0(2), n0(3)), v("sn", 0, S)), "send1": (send, 1, cut(8), cut(4)),
-             "send2": (send, 2, v("U", n0(2), n0(3)), v("cf", 2 * S, 3 * S)), "send3": (send, 3, cut(9), cut(7)),
-             "send4": (send, 4, v("P", n0(5), n0(6)), v("sn", S, 2 * S)),
-             "fold0": (fold, 0, slots("A0", 0, 512)), "fold1": (fold, 1, slots("A1", 0, 512)), "fold2": (fold, 2, slots("A3", 0, 512)),
-             "fold3": (fold, 3, slots("A2", 0, 512, (3, 4))), "fold4": (fold, 4, slots("A0", 0, 512)),
-             "upper2": (upper, 2, 0, 512, 256), "upper5": (upper, 5, 768, 1280, 1024),
-             "ym0": (out, T.ym, 0, 0), "ym1": (out, T.ym, 1, 512), "ym3": (out, T.ym, 3, 768), "ym4": (out, T.ym, 4, 1280),
-             "yz0": (out01,), "yz2": (out, T.yz, 2, 2048, 2), "yz4": (out_t, 4, 3072)}
-    for k in range(2):
-        piece["first%d" % k] = (first, k)
-        piece["firstf%d" % k] = (cp, v("cf", k * S, k * S + S), cut(k))
-    for m in range(6):
-        for nm, fn in (("prep", prep), ("elect", elect), ("won", won), ("keep", keep), ("snap", snap), ("col", column), ("place", place),
-                       ("twins", twins), ("ext", extend), ("neg", neg_p)):
-            piece["%s%d" % (nm, m)] = (fn, m)
-        for u in range(4):
-            piece["c%du%d" % (m, u)] = (unit, "c%d" % m, u)
-            piece["c%ds%d" % (m, u)] = (score, m, u)
-            piece["c%de%d" % (m, u)] = (exp_c, m, u)
-            piece["r%du%d" % (m, u)] = (unit, "r%d" % m, u) if m in (2, 4, 5) else (unit_r, m, {0: Q0, 1: Q1, 3: Q4}[m][u])
-        for h in range(2):
-            piece["c%dg%d" % (m, h)] = (gather, "c%d" % m, 2 * h, 2)
-            piece["r%dg%d" % (m, h)] = (gather, "r%d" % m, 2 * h, 2)
-        for q in range(4):
-            piece["c%dq%d" % (m, q)] = (gather, "c%d" % m, q)
-            piece["r%dq%d" % (m, q)] = (gather, "r%d" % m, q)
-    for u in range(4):
-        piece["r0e%d" % u] = (exp_r, "A2", Q0[u], 0, S)
-        piece["r1e%d" % u] = (exp_r, "A2", Q1[u], S, 2 * S)
-        piece["r23e%d" % u] = (exp_r, "A0", Q4[u], 0, 2 * S)
-        piece["r4e%d" % u] = (sum_t, 4, u)
-        piece["last%d" % u] = (last, u)
+    do("load", load)
+    scores(0), extend(0), elect(0), column(0)
+    scores(2), elect(2)
+    scores(1), extend(1), elect(1), column(1)
+    extend(2), column(2)
+    do("exp0", exp_c, 0), do("exp2", exp_c, 2), do("fold0", fold, 0), out(T.ym, 0, 0)
+    sizes(0, (3, 4))
+    scores(3), extend(3), elect(3), column(3)
+    do("exp1", exp_c, 1), do("exp3", exp_c, 3), do("fold1", fold, 1), out(T.ym, 1, 512), out(T.ym, 3, 768)
+    sizes(1, (4,)), by_maxima(0, 1)
+    do("read01", exp_r, 0, 1, [i for i in range(16) if i not in (3, 4)]), do("fold2", fold, 2)
+    scores(5), scores(4), extend(4), elect(5), elect(4), column(4), extend(5), column(5)
+    sizes(2), sizes(3), by_maxima(2, 3)
+    do("again", again), out(T.yz, 0, 1024, 2)
+    do("exp5", exp_c, 5), do("exp4", exp_c, 4), do("fold3", fold, 3), do("fold4", fold, 4), out(T.ym, 4, 1792)
+    do("upper2", upper, 2, 0, 512, 256), do("upper5", upper, 5, 768, 1792, 1536)
+    do("read23", exp_r, 2, 3, range(16)), do("fold5", fold, 5), do("fold6", fold, 6)
+    sizes(4), sizes(5), by_maxima(4, 5)
+    do("tail", tail)
+    do("join", tt, v("R", 0, 512), v("R", 0, 512), v("R", 2048, 2560), A.add), out(T.yz, 2, 0, 2)
 
-    def woven(m, name, h):
-        a = len(ops)
-        extend(m)
-        b = len(ops)
-        gather(name, 2 * h, 2, 16)
-        ops[a:] = [o for pair in zip(ops[b:], ops[b - 16:b]) for o in pair]
-
-    def step(fn, m, k, n=1):
-        a = len(ops)
-        fn(m)
-        ops[a:] = ops[a + k:a + k + n]
-
-    for m, name, h in WOVEN:
-        piece["ext%d" % m] = (woven, m, name, h)
-        for k in range(5):
-            piece["elect%d%s" % (m, "abcde"[k])] = (step, elect, m, k, 3 if k == 4 else 1)
-        for k in range(4 if m in (0, 1, 4) else 5):
-            piece["ext%d%s" % (m, "abcde"[k])] = (step, extend, m, k)
-        for k in range(2):
-            piece["snap%d%s" % (m, "ab"[k])] = (step, snap, m, k)
-        for k in range(16):
-            piece["sc%d%s" % (m, "abcdefghijklmnop"[k])] = (step, extend, m, k + (4 if m in (0, 1, 4) else 5))
-        for k in range(8):
-            piece["%so%d" % (name, k)] = (gather, name, k / 2, 0.5)
-    for name in ORDER:
-        piece[name][0](*piece[name][1:])
-
-    hist = {}
+    if not PLAN:
+        deps = overlap_deps(ops, range(len(ops)), regs, False)
+        for k, o in enumerate(ops):
+            deps[k] |= set(o["follows"])
+        PLAN["ops"], PLAN["d0"] = ops, deps
+        PLAN["order"], PLAN["ring"], PLAN["took"] = plan(ops, deps)
+    ring.update(PLAN["ring"])
     for k, o in enumerate(ops):
-        deps = set()
-        for kind, regs in (("r", o["r"]), ("w", o["w"])):
-            for e in regs:
-                name, lo, hi = e[:3]
-                for k2, kind2, lo2, hi2 in hist.get(name, ()):
-                    if lo < hi2 and lo2 < hi:
-                        o2 = ops[k2]
-                        same = o2["q"] == o["q"] and o2["sem"] is None and o["sem"] is None
-                        if name == "ps" and not same:
-                            deps.add(k2)
-                        elif "w" in (kind, kind2) and not (same and o["q"] == "pe"):
-                            deps.add(k2)
-        o["deps"] = deps if o["q"] != "far" else set()
-        for kind, regs in (("r", o["r"]), ("w", o["w"])):
-            for e in regs:
-                name, lo, hi = e[:3]
-                h = hist.setdefault(name, [])
-                if name == "ps":
-                    h[:] = [x for x in h if not (x[2] == lo and ops[x[0]]["q"] == o["q"] and (x[1] == "r" or kind == "w"))]
-                h.append((k, kind, lo, hi))
+        if PLAN["took"][k] != o["q"]:
+            o["q"], o["fn"], o["was"] = "act", [o["alt"]], "dve"
+    if "deps" not in PLAN:
+        PLAN["deps"] = overlap_deps(ops, PLAN["order"], regs, True)
+    order, deps = PLAN["order"], PLAN["deps"]
+
     needed = set()
-    for o in ops:
-        needed |= o["deps"]
+    for k in order:
+        if ops[k]["q"] != "far":
+            needed |= deps[k]
     count = {}
-    for k, o in enumerate(ops):
+    for k in order:
+        o = ops[k]
         if o["sem"] is not None:
             o["done"] = (o["sem"], abs(o["inc"]))
         elif k in needed:
@@ -537,12 +683,14 @@ def rank_program(g, core, T, topo):
             o["done"] = (o["q"], count[o["q"]])
     queue = {"pe": g.tensor, "act": g.scalar, "dve": g.vector, "pool": g, "sp": g.sync}
     known = {q: {} for q in queue}
-    for k, o in enumerate(ops):
+    place = {k: j for j, k in enumerate(order)}
+    for k in order:
+        o = ops[k]
         if o["q"] == "far":
             o["clock"] = {}
             continue
         kn = known[o["q"]]
-        for d in sorted(o["deps"], reverse=True):
+        for d in sorted(deps[k], key=lambda d: -place[d]):
             s, n = ops[d]["done"]
             if kn.get(s, 0) < n:
                 queue[o["q"]].wait_ge(T.sem[s], n)
@@ -550,7 +698,8 @@ def rank_program(g, core, T, topo):
                 for s2, n2 in ops[d]["clock"].items():
                     kn[s2] = max(kn.get(s2, 0), n2)
         o["clock"] = dict(kn)
-        ins = o["fn"]()
+        for fn in o["fn"]:
+            ins = fn()
         if "done" in o and o["inc"] > 0:
             ins.then_inc(T.sem[o["done"][0]], o["inc"])
     for o in ops:

import math
from concourse.bass import DstId, RemoteDMATransfer
from concourse.mybir import AluOpType as A, ActivationFunctionType as AF

F, S, OFF = 1984, 256, 16
W = F + 6 * S


def n0(m):
    return F + m * S


SCRATCH = {
    "P": ("sbuf", [128, W], "int32"),
    "U": ("sbuf", [128, OFF + n0(4)], "int32"),
    "str": ("sbuf", [128, 32], "int32"),
    "hvr": ("sbuf", [128, 16], "bfloat16"),
    "lnh": ("sbuf", [128, 48], "float32"),
    "nx": ("sbuf", [128, 4 * S], "float16"),
    "nP": ("sbuf", [128, 6 * S], "float16"),
    "Pg0": ("sbuf", [128, 4096], "float16"), "Pg1": ("sbuf", [128, 4096], "float16"), "Pg2": ("sbuf", [128, 4096], "float16"),
    "mx": ("sbuf", [128, 4096], "float16"), "Pr": ("sbuf", [128, 3 * S], "float16"),
    "A0": ("sbuf", [128, 16, 512], "float32"), "A1": ("sbuf", [128, 16, 512], "float32"),
    "A2": ("sbuf", [128, 16, 512], "float32"), "A3": ("sbuf", [128, 16, 512], "float32"),
    "R": ("sbuf", [128, 14 * S], "float32"),
    "cu": ("sbuf", [128, 10 * S], "uint16"),
    "ch": ("sbuf", [128, 2 * S], "float16"),
    "sn": ("sbuf", [128, 2 * S], "int32"),
    "obu": ("sbuf", [128, 8 * 16], "uint16"), "obh": ("sbuf", [128, 6 * 16], "float16"),
    "so": ("sbuf", [128, 32], "uint16"),
    "e1": ("sbuf", [128, S], "float32"), "e2": ("sbuf", [128, S], "float32"), "e3": ("sbuf", [128, S], "float32"),
    "e4": ("sbuf", [128, S], "float32"), "e5": ("sbuf", [128, S], "float32"),
    "pr": ("sbuf", [128, S], "float32"), "ua": ("sbuf", [128, S], "int32"), "sm": ("sbuf", [128, 32], "float32"), "ru": ("sbuf", [128, 48], "uint16"),
    "Nm": ("sbuf", [128, 6 * S], "int32"), "Dm": ("sbuf", [128, 15 * 128], "bfloat16"), "xd": ("sbuf", [128, 128], "bfloat16"),
    "I32": ("sbuf", [128, 128], "float32"), "Jb": ("sbuf", [128, 128], "bfloat16"), "Ib": ("sbuf", [128, 6 * 128], "bfloat16"),
    "jr": ("sbuf", [128, S], "float32"), "dl": ("sbuf", [128, S], "float32"), "big": ("sbuf", [128, S], "bfloat16"),
    "one": ("sbuf", [128, S], "bfloat16"), "dmk": ("sbuf", [128, S], "bfloat16"), "c2k": ("sbuf", [128, S], "bfloat16"),
    "hf": ("sbuf", [128, 64], "bfloat16"),
    "blk": ("sbuf", [128, 16], "float32"), "ci": ("sbuf", [128, 32], "int32"), "cfl": ("sbuf", [128, 16], "float32"),
    "bco": ("sbuf", [128, 16], "uint16"), "rdo": ("sbuf", [128, 4], "uint16"),
    "ps": ("psum", [128, 4096], "float32"),
}
FOLDS = (("A0", range(16), 0, 512, 0), ("A1", range(16), 0, 512, 512), ("A2", (0, 1, 2) + tuple(range(5, 16)), 0, 512, 1024),
         ("A3", range(16), 0, 256, 1536), ("A3", range(16), 256, 256, 1792), ("A0", range(8), 0, 512, 2048), ("A0", range(8, 16), 0, 512, 0))
NFOLD = len(FOLDS)
NARROW = ()
BEHIND = {5: (3,)}
SEMAPHORES = (["pe", "act", "dve", "pool", "hl"] + ["d%d" % k for k in range(20)] + ["l%d" % k for k in range(12)]
              + ["f%d" % k for k in range(NFOLD)] + ["b%d" % k for k in range(NFOLD)] + ["a%d" % k for k in range(4)])
LODGE = {"xa": ("P", n0(0)), "xb": ("P", n0(3)), "TT": ("Nm", 0), "t1": ("jr", 0), "xt2": ("nP", 3 * S), "xt5": ("Pr", 0)}
BYTES = {"float32": 4, "int32": 4, "float16": 2, "bfloat16": 2, "uint16": 2}
RING = (0, 1024, 2048)
KEY = (3072, 3584)
TAIL_PE = (0, 5, 10)
CUT = {"c0": 4, "c1": 8, "c3": 8, "c4": 8, "r4": 8, "r5": 4, "c2": 8, "c5": 16, "r2": 16}
PG = {"c0": "Pg0", "c2": "Pg1", "c1": "Pg2", "c3": "Pg0", "c5": "Pg1", "c4": "Pg2", "r2": "Pg0", "r4": "Pg1", "r5": "Pg0",
      "r0": "Pg2", "r1": "Pg0", "r3": "Pg2"}
BY_MAX = {(2, 3): (12, 16), (4, 5): (8, 16)}
EXP_CALLS = 2
DUE = {"sc5": -34, "size2": -19, "again": -13, "size4": -2, "fold6": 7, "max4": 35, "out": 48}
CYCLE, PE_CYCLE, GATHER, SCATTER, CALL, WAKE, DMA_FIX, DMA_RATE = 0.83, 0.38, 1.3, 3.5, 50.0, 170.0, 1800.0, 560.0
PATIENCE, HELP = 0.3, 0.8
PLAN = {}


def helper_of(core, T, topo):
    near = [c for c in topo.cores_of(core) if c != core and T.rank_of(c) is None and topo.die(c) == topo.die(core)]
    return min(near, key=lambda c: abs(c - core))


def fold_mask(k, core, T, topo):
    mk = topo.mask(core, helper_of(core, T, topo))
    return mk & ~topo.mask(core, T.cores[(T.rank_of(core) + 1) % len(T.cores)]) if k in NARROW else mk


def bits(m):
    return bin(m).count("1")


def overlap_deps(ops, order, regs, banks):
    hist, deps = {}, {}
    for k in order:
        o, d = ops[k], set()
        touched = [("r", e) for x in o["r"] for e in regs(x)] + [("w", e) for x in o["w"] for e in regs(x)]
        for kind, (name, lo, hi) in touched:
            for k2, kind2, lo2, hi2 in hist.get(name, ()):
                o2 = ops[k2]
                same = o2["q"] == o["q"] and o2["sem"] is None and o["sem"] is None
                if banks and name == "ps" and not same and lo // 512 <= (hi2 - 1) // 512 and lo2 // 512 <= (hi - 1) // 512:
                    d.add(k2)
                elif lo < hi2 and lo2 < hi and "w" in (kind, kind2) and not (banks and same and o["q"] == "pe"):
                    d.add(k2)
        for kind, (name, lo, hi) in touched:
            h = hist.setdefault(name, [])
            if kind == "w":
                h[:] = [x for x in h if not (lo <= x[2] and x[3] <= hi and (x[0] in d or x[0] == k))]
            h.append((k, kind, lo, hi))
        deps[k] = d
    return deps


def plan(ops, deps):
    n, first = len(ops), {}
    deps = [set(deps[k]) for k in range(n)]
    for k, o in enumerate(ops):
        for u in o["units"]:
            if first.setdefault(u, k) != k:
                deps[first[u]] |= {d for d in deps[k] if u not in ops[d]["units"]}
    after = [[] for _ in range(n)]
    for k in range(n):
        for d in deps[k]:
            after[d].append(k)
    urgency, seen = [0.0] * n, [False] * n

    def weigh(k):
        if not seen[k]:
            seen[k] = True
            urgency[k] = max([-1000.0 * DUE.get(ops[k]["piece"], 200)] + [weigh(j) + WAKE for j in after[k]]) + ops[k]["hold"] + ops[k]["lat"]
        return urgency[k]
    for k in range(n - 1, -1, -1):
        weigh(k)
    left = [len(deps[k]) for k in range(n)]
    ready, took = {"act": {}}, {}
    for k in range(n):
        if not left[k]:
            ready.setdefault(ops[k]["q"], {})[k] = 0.0
    free, order, ring, ring_free, users, end = {}, [], {}, {b: 0.0 for b in RING}, {}, [0.0] * n
    for o in ops:
        for u in o["units"]:
            users[u] = users.get(u, 0) + 1
    while len(order) < n:
        best = None
        for q, rq in ready.items():
            cand, fq = [], free.get(q, 0.0)
            for k, t in rq.items():
                o = ops[k]
                if o["units"] and any(u not in ring for u in o["units"]):
                    if not ring_free:
                        continue
                    t = max(t, min(ring_free.values()))
                for e in o["eng"]:
                    t = max(t, free.get(e, 0.0))
                cand.append((max(t, fq), k))
            if q == "act":
                mine = min(cand)[0] if cand else 1e9
                cand += [(max(t, fq), k) for k, t in ready.get("dve", {}).items() if ops[k]["alt"] and max(t, fq) + HELP * ops[k]["hold"] < mine]
            if not cand:
                continue
            t0 = min(cand)[0]
            k = max((k for t, k in cand if t == t0), key=lambda k: urgency[k])
            while True:
                span = PATIENCE * max([ops[k]["hold"]] + list(ops[k]["eng"].values()))
                soon = [(t, j) for t, j in cand if t < t0 + span and urgency[j] > urgency[k] + span]
                if not soon:
                    break
                t0, k = max(soon, key=lambda x: urgency[x[1]])
            if best is None or (t0, q == "act") < (best[0], best[2] == "act"):
                best = (t0, k, q)
        t0, k, q = best
        o = ops[k]
        del ready[o["q"]][k]
        order.append(k)
        took[k] = q
        free[q] = t0 + o["hold"]
        for e, d in o["eng"].items():
            free[e] = t0 + d
        end[k] = t0 + o["hold"] + o["lat"]
        for u in o["units"]:
            if u not in ring:
                ring[u] = min(ring_free, key=lambda b: ring_free[b])
                del ring_free[ring[u]]
            users[u] -= 1
            if not users[u]:
                ring_free[ring[u]] = end[k] + WAKE
        for j in after[k]:
            left[j] -= 1
            if not left[j]:
                ready.setdefault(ops[j]["q"], {})[j] = max(end[d] for d in deps[j]) + WAKE
    order.sort(key=lambda k: (0, k) if ops[k]["sem"] and not deps[k] else (1, 0))
    PLAN["end"] = end
    return order, ring, took


def rank_program(g, core, T, topo):
    rank = T.rank_of(core)
    if rank is None:
        for owner in T.cores:
            if helper_of(owner, T, topo) == core:
                rid, pid = topo.addr(owner)[:2]
                m_out = topo.mask(core, owner)
                for k in range(NFOLD):
                    x = T.R[:, FOLDS[k][4]:FOLDS[k][4] + FOLDS[k][3]]
                    g.wait_ge(T.sem["f%d" % k], bits(fold_mask(k, owner, T, topo)))
                    g.remote_dma(x, x, T.sem["b%d" % k], T.sem.hl, pid, rid, m_out)
                g.wait_ge(T.sem.hl, NFOLD * bits(m_out))
        return
    N = len(T.cores)
    nxt, prv, hlp = T.cores[(rank + 1) % N], T.cores[(rank - 1) % N], helper_of(core, T, topo)
    ops, ring, tag = [], {}, [None]

    def v(name, lo=None, hi=None, step=1, rows=None, unit=None):
        if name in LODGE:
            name, lo, hi = LODGE[name][0], LODGE[name][1] + lo, LODGE[name][1] + hi
        if lo is None:
            lo, hi = 0, SCRATCH[name][1][1]
        n = len(range(lo, hi, step)) * (rows[1] - rows[0] if rows else 1)
        return {"name": name, "lo": lo, "hi": hi, "step": step, "rows": rows, "unit": unit, "off": None, "n": n, "b": BYTES[SCRATCH[name][2]]}

    def v3(name, i0, i1, lo, hi):
        return v(name, lo, hi, rows=(i0, i1))

    def ind(win, off):
        return dict(win, off=off, n=16 * off["n"])

    def hbm(t, n, reg=None):
        return {"name": None, "ap": t, "off": None, "unit": None, "n": n, "b": 4, "reg": [reg] if reg else []}

    def ap(x):
        if not isinstance(x, dict):
            return x
        if x["name"] is None:
            return x["ap"]
        t, b = T[x["name"]], ring[x["unit"]] if x["unit"] is not None else 0
        if x["rows"]:
            i0, i1 = x["rows"]
            return t[:, i0, x["lo"]:x["hi"]] if i1 == i0 + 1 else t[:, i0:i1, x["lo"]:x["hi"]]
        a = t[:, b + x["lo"]:b + x["hi"]] if x["step"] == 1 else t[:, b + x["lo"]:b + x["hi"]:x["step"]]
        return a.indirect(ap(x["off"])) if x["off"] else a

    def regs(x):
        if x["name"] is None:
            return x["reg"]
        if x["rows"]:
            return [(x["name"], i * 512 + x["lo"], i * 512 + x["hi"]) for i in range(*x["rows"])]
        if x["unit"] is None:
            return [(x["name"], x["lo"], x["hi"])]
        if ring:
            return [("ps", ring[x["unit"]] + x["lo"], ring[x["unit"]] + x["hi"])]
        return [("unit%d" % x["unit"], x["lo"] // 512 * 512, (x["hi"] + 511) // 512 * 512)]

    def op(q, fn, reads, writes, hold, sem=None, inc=1, lat=0.0, join=False, follows=(), eng=None):
        rr = [x for x in reads if isinstance(x, dict)]
        rr += [x["off"] for x in rr + writes if x["off"]]
        units = {x["unit"] for x in rr + writes if x["unit"] is not None}
        if q in ("pe", "act", "dve"):
            eng = {"bank%d" % (x["lo"] // 512): hold for x in rr + writes if x["name"] == "ps" and x["unit"] is None}
        if join:
            o = ops[-1]
            o["fn"].append(fn)
            o["r"] += rr
            o["w"] += writes
            o["hold"] += hold
            o["units"] |= units
            o["eng"] = {e: o["hold"] for e in list(o["eng"]) + list(eng)}
        else:
            ops.append({"q": q, "fn": [fn], "r": rr, "w": list(writes), "sem": sem, "inc": inc, "hold": hold, "lat": lat, "units": units,
                        "follows": list(follows), "eng": eng or {}, "piece": tag[0], "alt": None})
        return len(ops) - 1

    def mm(out, l, r, start, stop, join=False):
        op("pe", lambda: g.tensor.matmul(ap(out), ap(l), ap(r), start, stop), [l, r], [out],
           max(min(64, l["n"]), r["n"]) * (4 if l["b"] == 4 else 1) * PE_CYCLE, join=join)

    def vec(fn, reads, out, two=False):
        wide = [x for x in reads + [out] if isinstance(x, dict) and x["n"] == out["n"]]
        if out["off"] or any(x["off"] for x in wide):
            hold = CALL + out["n"] * (SCATTER if out["off"] else GATHER)
        else:
            hold = CALL + max(64, out["n"] * (0.5 if all(x["b"] == 2 for x in wide) else 1) * (2 if two else 1)) * CYCLE
        op("dve", fn, reads, [out], hold)

    def cp(out, a):
        vec(lambda: g.vector.tensor_copy(ap(out), ap(a)), [a], out)

    def tt(out, a, b, o):
        vec(lambda: g.vector.tensor_tensor(ap(out), ap(a), ap(b), o), [a, b], out, "ps" not in (a["name"], b["name"]))

    def ts(out, a, s1, o0, s2=None, o1=None):
        if o1 is None:
            vec(lambda: g.vector.tensor_scalar(ap(out), ap(a), ap(s1), None, o0), [a, s1], out)
        else:
            vec(lambda: g.vector.tensor_scalar(ap(out), ap(a), ap(s1), ap(s2), o0, o1), [a, s1, s2], out)

    def affine(out, a, scale, bias):
        ts(out, a, scale, A.mult, bias, A.add)
        ops[-1]["alt"] = lambda: g.scalar.activation(ap(out), ap(a), AF.Identity, bias=bias, scale=scale)

    def scan(out, d0, d1, o0, o1):
        vec(lambda: g.vector.tensor_tensor_scan(ap(out), ap(d0), ap(d1), 0.0, o0, o1), [d0, d1], out)

    def turn(out, a):
        vec(lambda: g.vector.transpose(ap(out), ap(a)), [a], out)

    def fill(out, c):
        vec(lambda: g.vector.memset(ap(out), c), [], out)

    def act(out, a, f, bias=0.0, scale=1.0):
        op("act", lambda: g.scalar.activation(ap(out), ap(a), f, bias=ap(bias), scale=ap(scale)), [a, bias, scale], [out], 2 * CALL + out["n"] * CYCLE)

    def iota(out, pat, base, cm):
        if SCRATCH[out["name"]][2] == "int32":
            op("pool", lambda: g.iota(ap(out), pat, base, cm), [], [out], 130 + 2 * out["n"] * CYCLE)
        else:
            op("pool", lambda: g.iota(ap(out), pat, base, cm, allow_small_or_imprecise_dtypes=True), [], [out], 130 + 2 * out["n"] * CYCLE)

    def sel(out, pat, cmp, fl, base=0):
        op("pool", lambda: g.affine_select(ap(out), ap(out), pat, cmp, fl, base, 1), [out], [out], 170 + 2 * out["n"] * CYCLE)

    nd, nl, last = [0], [0], {}

    def dma(q, out, a, behind=0):
        e = g.sync if q == "sp" else g.scalar
        op(q, lambda: e.dma_start(ap(out), ap(a)), [a], [out], 0, sem="d%d" % nd[0], inc=16,
           lat=DMA_FIX + 128 * (out["n"] * out["b"] + behind) / DMA_RATE)
        nd[0] += 1

    def send(k, out, a):
        rid, pid = topo.addr(nxt)[:2]
        mk, ls = topo.mask(core, nxt), "l%d" % nl[0]
        nl[0] += 1
        j = op("pool", lambda: g.remote_dma(ap(out), ap(a), T.sem["a%d" % k], T.sem[ls], pid, rid, mk), [a], [], 300, sem=ls, inc=-bits(mk),
               lat=1.5 * DMA_FIX, eng={"out": DMA_FIX / 2})
        last[k] = j
        op("far", None, [], [out], 0, sem="a%d" % k, inc=bits(topo.mask(prv, core)), lat=DMA_FIX / 2, follows=[j])

    def fold(k):
        rid, pid = topo.addr(hlp)[:2]
        mk, ls = fold_mask(k, core, T, topo), "l%d" % nl[0]
        nl[0] += 1
        an, slots, lo, n, c = FOLDS[k]
        out, srcs = v("R", c, c + n), [v3(an, i, i + 1, lo, lo + n) for i in slots]
        used = [out] if c in [x[4] for x in FOLDS[:k]] else []
        span = 128 * len(srcs) * (4 * n + 600) / DMA_RATE * (2 if k in NARROW else 1)
        last["fold"] = op("pool", lambda: g.remote_dma_fused([RemoteDMATransfer(
            dst_ids=[DstId(rid=rid, pnc=pid)], dma_engine_mask=mk, remote_sem=T.sem["f%d" % k],
            srcs=[ap(s) for s in srcs], dsts=[ap(out)], alu_op=1)], local_sem=T.sem[ls]), srcs, used, 300, sem=ls, inc=-bits(mk),
            lat=DMA_FIX + span, follows=[last[x] for x in ("fold",) + BEHIND.get(k, ()) if x in last], eng={"in": span} if k in NARROW else {"in": span, "out": span})
        op("far", None, [], [out], 0, sem="b%d" % k, inc=bits(topo.mask(hlp, core)), lat=1.5 * DMA_FIX, follows=[last["fold"]])

    LEVEL = [0, 0, 1, 0, 0, 1]
    TIMES = [[0], [1], [0, 1], [2], [3], [2, 3]]
    CAND = [0, 2, 1, 3, 5, 4]
    RCU = [2, 3, 8, 5, 6, 9]
    NWIN = [n0(0), n0(1), n0(0), n0(2), n0(4), n0(3)]
    XWIN = [n0(0), n0(0), n0(0), n0(2), n0(2), n0(0)]
    AB = {"c0": ("A0", 0), "c2": ("A0", S), "c1": ("A1", 0), "c3": ("A1", S), "r0": ("A2", 0), "r1": ("A2", S),
          "c5": ("A3", 0), "c4": ("A3", S), "r2": ("A0", 0), "r3": ("A0", S), "r4": ("A1", 0), "r5": ("A1", S)}
    SCALES = (1.0, 0.5, -0.25, -0.125, -1.0, -2.0)
    I1, IH, IQ, IE, IN, I2 = (v("Ib", k * 128, k * 128 + 128) for k in range(6))
    qf = v("cfl", 0, 1)
    nu = [0]

    def buf():
        nu[0] += 1
        u = nu[0]
        return lambda lo, hi, step=1: v("ps", lo, hi, step, unit=u)

    def cut(k, lo=0, hi=S):
        return v("cu", k * S + lo, k * S + hi)

    def ob(kind, k):
        return v("ob" + kind, k * 16, k * 16 + 16)

    def succ(lo, hi):
        return v("U", OFF + lo, OFF + hi)

    def sym(t, lo=0, hi=S):
        return v("nx", t // 2 * 2 * S + 2 * lo + t % 2, t // 2 * 2 * S + 2 * hi, 2)

    def do(piece, fn, *a):
        tag[0] = piece
        fn(*a)

    def load():
        dma("act", v("hvr"), hbm(T.hv[:], 16))
        dma("sp", v("str"), hbm(T.st[:], 32))
        dma("act", succ(0, F), hbm(T.su[:], F))
        dma("sp", v("P", 0, F), hbm(T.th[:], F), 4 * F)
        dma("act", v("xa", 0, 2 * S), hbm(T.xs[:, 0:2 * S], 2 * S), 8 * F)
        dma("sp", v("xb", 0, 2 * S), hbm(T.xs[:, 2 * S:4 * S], 2 * S), 8 * F + 8 * S)
        fill(v("I32"), 1.0)
        fill(v("Jb"), 1.0)
        fill(v("c2k"), 2048.0)
        fill(v("U", 0, OFF), 0)
        iota(v("ci", 0, 1), [[0, 1]], 0, 1)
        iota(v("jr"), [[0, 16], [1, 16]], 0, 0)
        sel(v("I32"), [[-1, 128]], A.is_equal, 0.0)
        sel(v("Jb"), [[-16, 8], [1, 16]], A.is_equal, 0.0, -15)
        iota(v("ci", 16, 32), [[16, 16]], 15, 0)
        iota(v("e1"), [[1, S]], n0(0), 0)
        iota(v("e2", 0, 128), [[1, 8], [0, 16]], 0, 0)
        ts(v("ci", 1, 2), v("ci", 0, 1), 15, A.bitwise_and)
        ts(v("ci", 2, 3), v("ci", 0, 1), 4, A.logical_shift_right)
        ts(v("big"), v("jr"), 0.0, A.is_equal, 2.0 ** 40, A.mult)
        cp(v("cfl", 0, 2), v("ci", 1, 3))
        tt(v("ci", 3, 4), v("ci", 0, 1), v("ci", 2, 3), A.add)
        ts(v("one"), v("jr"), 0.0, A.is_equal)
        ts(v("ci", 4, 5), v("ci", 3, 4), 1, A.bitwise_and)
        ts(v("dl"), v("jr"), qf, A.is_equal)
        ts(v("cfl", 2, 3), v("ci", 4, 5), 33.0, A.mult, qf, A.add)
        ts(v("dmk"), v("jr"), qf, A.is_gt, 64.0, A.mult)
        for k, c in enumerate((3.0, 4.0, 260.0)):
            ts(v("rdo", k, k + 1), v("cfl", 2, 3), 16.0, A.mult, c, A.add)
        ts(v("blk", 0, 8), v("jr", 0, 8), v("cfl", 1, 2), A.is_equal)
        ts(v("blk", 8, 16), v("jr", 0, 8), v("cfl", 1, 2), A.is_equal, 2.0 ** 13, A.mult)
        cp(v("bco"), v("ci", 16, 32))
        ts(v("cfl", 3, 4), qf, float(S), A.mult)
        ts(v("e1"), v("e1"), v("cfl", 3, 4), A.add)
        ts(v("e2", 0, 128), v("e2", 0, 128), v("cfl", 1, 2), A.is_equal)
        tt(v("xd"), v("e2", 0, 128), v("I32"), A.add)
        ts(v("e4", 0, 16), v("dl", 0, 16), -1.0, A.mult, 2.0, A.add)
        ts(v("e4", 16, 32), v("dl", 0, 16), -2.0 / 64, A.mult, 1.0 / 64, A.add)
        for j in range(15):
            ts(v("Dm", j * 128, j * 128 + 128), v("xd"), v("e4", j, j + 1), A.is_equal, v("e4", 16 + j, 17 + j), A.mult)
        cp(v("obu", 0, 32), v("str"))
        ts(v("obh", 0, 32), v("str"), -2048.0, A.add)
        for k, c in enumerate(SCALES):
            act(v("Ib", k * 128, k * 128 + 128), v("I32"), AF.Copy, scale=c)
        tt(v("hf"), v("Ib", 128, 256, 2), v("Ib", 129, 256, 2), A.add)
        for m in range(6):
            act(v("Nm", m * S, m * S + S), v("e1"), AF.Copy, scale=v("dl", m, m + 1))
        tag[0] = "ln"
        y, e = v("lnh", 16, 32), v("lnh", 32, 48)
        ts(y, v("hvr"), 0.9, A.mult, -1.05, A.add)
        for k in range(4):
            act(e, y, AF.Exp, bias=float(k), scale=-1.0)
            tt(e, e, v("hvr"), A.mult)
            tt(y, y, e, A.add)
        ts(v("lnh", 0, 16), y, -4.0 - math.log(16.0), A.add)
        tag[0] = "load"
        for k in range(2):
            cp(cut(k), ind(succ(0, F), ob("u", k)))
        for t in range(4):
            affine(sym(t), v("xb" if t > 1 else "xa", t % 2 * S, t % 2 * S + S), -1.0, 2048.0)

    def gather(name):
        m, n = int(name[1]), S // CUT[name]
        k, w = (CAND[m], NWIN[m]) if name[0] == "c" else (RCU[m], n0(m + 1))
        for s in range(0, S, n):
            affine(v(PG[name], s * 16, (s + n) * 16), ind(v("P", 0, w), cut(k, s, s + n)), 1.0, -2048.0)

    def unit(name, s0, s1, i0, i1):
        m, b, n = int(name[1]), buf(), s1 - s0
        for i in range(i0, i1):
            o = b((i - i0) * n, (i - i0 + 1) * n)
            mm(o, I1, v(PG[name], s0 * 16 + i, s1 * 16, 16), True, False, join=(i - i0) * n % 512 > 0)
            if name[0] == "r":
                mm(o, I1, v("nP", m * S + s0, m * S + s1), False, True, join=True)
            elif LEVEL[m]:
                mm(o, v("xt%d" % m, 2 * s0, 2 * s1), v("hf"), False, True, join=True)
            else:
                mm(o, I1, sym(TIMES[m][0], s0, s1), False, True, join=True)
        an, ao = AB[name]
        act(v3(an, i0, i1, ao + s0, ao + s1), b(0, (i1 - i0) * n), AF.Abs)

    def scores(m):
        name, kb, lv = "c%d" % m, KEY[LEVEL[m]], LEVEL[m]
        an, ao = AB[name]
        do("g%d" % m, gather, name)
        tag[0] = "sc%d" % m
        ts(v("ch", lv * S, lv * S + S), cut(CAND[m]), -2048.0, A.add)
        mm(v("ps", kb + S, kb + 2 * S), I1, v("c2k"), True, False)
        for h in range(2):
            mm(v("ps", kb + S + h * 128, kb + S + h * 128 + 128), v("ch", lv * S + h * 128, lv * S + h * 128 + 128), v("Jb"), False, h == 1, join=True)
        if lv:
            b, t = buf(), TIMES[m][0]
            for q in range(4):
                mm(b(q * 128, q * 128 + 128), v("nx", t * S + q * 128, t * S + q * 128 + 128), I1, True, True, join=q > 0)
            act(v("xt%d" % m, 0, 512), b(0, 512), AF.Copy)
        for h in range(2):
            quarters = lv or (m == 0 and h == 0)
            if quarters:
                unit(name, h * 128, h * 128 + 64, 0, 16), unit(name, h * 128 + 64, h * 128 + 128, 0, 16)
            for i0 in (0, 8):
                if not quarters:
                    unit(name, h * 128, h * 128 + 128, i0, i0 + 8)
                for i in range(i0, i0 + 8):
                    mm(v("ps", kb + h * 128 + 15 - i, kb + h * 128 + 128, 16), v3(an, i, i + 1, ao + h * 128, ao + h * 128 + 128), v("blk", 8, 16),
                       True, True, join=i % 4 > 0)

    def exp_c(m):
        an, ao = AB["c%d" % m]
        n = 16 // EXP_CALLS
        for i in range(0, 16, n):
            x = v3(an, i, i + n, ao, ao + S)
            act(x, x, AF.Exp, bias=-math.log(16.0 * (1 + LEVEL[m])), scale=-1.0 / 512)

    def by_max(m):
        return [i for ms, (lo, hi) in BY_MAX.items() if m in ms for i in range(lo, hi)]

    def sizes(m, skip=()):
        name = "r%d" % m
        tag[0] = "size%d" % m
        affine(v("nP", m * S, m * S + S), v("P", n0(m), n0(m) + S), -1.0, 2048.0)
        slots = [i for i in range(16) if i not in skip and i not in by_max(m)]
        if name in CUT:
            do("rg%d" % m, gather, name)
            tag[0] = "size%d" % m
            for h in range(2):
                for j in range(0, len(slots), 8):
                    unit(name, h * 128, h * 128 + 128, slots[j], slots[j:j + 8][-1] + 1)
            return
        run = []
        for i in range(17):
            if run and (i not in slots or len(run) == 4):
                unit(name, 0, S, run[0], run[-1] + 1)
                run = []
            if i in slots:
                run.append(i)

    def maxima(ms):
        lo, hi = BY_MAX[ms]
        w = len(ms) * S
        for j, m in enumerate(ms):
            tag[0] = "max%d" % m
            x = buf()(0, S)
            mm(x, IN, v("nP", m * S, m * S + S), True, True)
            for i in range(lo, hi):
                tt(v("mx", (i - lo) * w + j * S, (i - lo) * w + j * S + S), v(PG["r%d" % m], i, 4096, 16), x, A.max)
        tag[0] = "mexp%d" % ms[0]
        for i0 in range(lo, hi, 1024 // w):
            b = buf()
            for i in range(i0, min(hi, i0 + 1024 // w)):
                o = (i - i0) * w
                mm(b(o, o + w), I2, v("mx", (i - lo) * w, (i - lo + 1) * w), True, False, join=o % 512 > 0)
                mm(b(o, o + w), IN, v("nP", ms[0] * S, ms[0] * S + w), False, False, join=True)
                for j, m in enumerate(ms):
                    mm(b(o + j * S, o + j * S + S), I1, v(PG["r%d" % m], i, 4096, 16), False, j == len(ms) - 1, join=True)
            an, ao = AB["r%d" % ms[0]]
            for i in range(i0, min(hi, i0 + 1024 // w)):
                act(v3(an, i, i + 1, ao, ao + w), b((i - i0) * w, (i - i0 + 1) * w), AF.Exp, bias=v("lnh", i, i + 1), scale=1.0 / 512)

    def by_maxima(ma, mb):
        for ms in BY_MAX:
            if ms[0] in (ma, mb):
                maxima(ms)

    def exp_r(ma, mb, slots):
        for i in slots:
            ms = [m for m in (ma, mb) if i not in by_max(m)]
            if ms:
                an, ao = AB["r%d" % ms[0]]
                x = v3(an, i, i + 1, ao, ao + len(ms) * S)
                act(x, x, AF.Exp, bias=v("lnh", i, i + 1), scale=-1.0 / 512)

    def elect(m):
        tag[0] = "el%d" % m
        kb, tm = KEY[LEVEL[m]], TIMES[m]
        key, low = v("ps", kb, kb + S), v("ps", kb + S, kb + 2 * S)
        scan(v("e1"), v("big"), key, A.add, A.min)
        tt(v("e2"), key, v("e1"), A.subtract)
        tt(v("e3"), low, v("e2"), A.subtract)
        for k, t in enumerate(tm):
            mm(low, IQ if len(tm) == 1 else IE, sym(t), k == 0, k == len(tm) - 1, join=k > 0)
        scan(v("e4"), v("e2"), v("e3"), A.min, A.max)
        tt(v("e5"), ind(v("e4"), v("bco")), v("dl"), A.mult)
        for h in range(2):
            mm(v("ps", kb + h * 8, kb + h * 8 + 8), v("e5", h * 128, h * 128 + 128), v("blk", 0, 8), True, True, join=h > 0)
        cp(ob("u", 2 + m), v("ps", kb, kb + 16))
        if m < 4:
            ts(ob("h", 2 + m), ob("u", 2 + m), -2048.0, A.add)
        affine(v("t1", 0, S), ind(v("P", 0, NWIN[m]), ob("u", 2 + m)), 0.75, 512.0 - (0.375 if LEVEL[m] == 0 else 0.4375))
        out = v("P", n0(m), n0(m) + S) if LEVEL[m] == 0 else v("sn", (m // 3) * S, (m // 3) * S + S)
        tt(out, low, v("t1", 0, S), A.add)
        if LEVEL[m]:
            send(m // 3 * 2, v("P", n0(m), n0(m + 1)), out)

    def column(m):
        tag[0] = "col%d" % m
        cp(cut(2 + m), ind(succ(0, NWIN[m]), ob("u", 2 + m)))
        if LEVEL[m]:
            send(m // 3 * 2 + 1, cut(RCU[m]), cut(2 + m))
        if m < 4:
            x, y = succ(n0(m), n0(m + 1)), cut(RCU[m])
            op("pool", lambda: g.affine_select(ap(x), ap(y), [[0, S]], A.is_equal, 0.0, 0, 0), [y], [x], 170 + 2 * S * CYCLE)

    def extend(m):
        tag[0] = "ext%d" % m
        tw = buf()
        mm(tw(0, S), I1, v("dmk"), True, False)
        for j in range(15):
            mm(tw(j + 1, S, 16), v("Dm", j * 128, j * 128 + 128), ob("h", CAND[m]), False, j == 14, join=True)
        scan(v("pr", 0, S), tw(0, S), v("one"), A.mult, A.add)
        tt(v("ua"), ind(succ(0, XWIN[m]), ob("u", CAND[m])), v("Nm", m * S, m * S + S), A.max)
        ts(v("sm", 0, 16), v("pr", 15, S, 16), 0.0, A.is_equal, -8192.0, A.mult)
        tt(v("sm", 16, 32), ob("h", CAND[m]), v("sm", 0, 16), A.add)
        ts(v("so", 0, 32, 2), v("sm", 16, 32), 2048.0 + OFF, A.add, qf, A.max)
        for c in range(15, -1, -1):
            cp(ind(v("U", 0, OFF + XWIN[m]), v("so", 2 * c, 2 * c + 1)), v("ua", c * 16, c * 16 + 16))

    def again():
        turn(v("TT", 0, 512), succ(n0(0), n0(2)))
        turn(v("TT", 512, 1056), succ(n0(0) - 16, n0(2) + 16))
        cp(v("ru"), ind(v("TT", 0, 1056), v("rdo", 0, 3)))
        affine(v("Pr"), ind(v("P", 0, n0(5)), v("ru")), 1.0, -2048.0)
        b = buf()
        for j, m in enumerate((0, 0, 1)):
            o = b(j * S, j * S + S)
            mm(o, I1, v("Pr", j * S, j * S + S), True, False, join=j > 0)
            mm(o, I1, v("nP", m * S, m * S + S), False, True, join=True)
        act(v3("A2", 3, 4, 0, S), b(0, S), AF.Abs)
        act(v3("A2", 4, 5, 0, 2 * S), b(S, 3 * S), AF.Abs)
        exp_r(0, 1, (3, 4))
        b = buf()(0, 512)
        for i in (3, 4):
            mm(b, v("I32"), v3("A2", i, i + 1, 0, 512), i == 3, i == 4)
        tt(v("R", 1024, 1536), b, v("R", 1024, 1536), A.add)

    def out(t, m, c, n=1, q="sp"):
        tag[0] = "out"
        dma(q, hbm(t[:, m * S:(m + n) * S], n * S, (t.name, m, m + n)), v("R", c, c + n * S))

    def upper(m, a, b, q):
        x, o = buf()(0, S), 2560 + (m // 3) * S
        ts(x, v("R", a, a + S), 0.5, A.mult)
        tt(x, x, v("R", b, b + S), A.mult)
        tt(v("R", o, o + S), x, v("R", q, q + S), A.add)
        out(T.ym, m, o)

    def tail():
        slots = sorted(range(16), key=lambda i: i in by_max(4))
        on_pe = [slots[k] for k in TAIL_PE]
        on_v = [i for i in slots if i not in on_pe]
        acc, sums, res = v("ps", KEY[1], KEY[1] + 512), v("ps", KEY[0], KEY[0] + 512), v("R", 3072, 3584)
        exp_r(4, 5, slots)
        for i in slots:
            x = v3("A1", i, i + 1, 0, 512)
            if i in on_pe:
                mm(sums, v("I32"), x, i == on_pe[0], i == on_pe[-1])
            elif i == on_v[0]:
                cp(acc, x)
            else:
                tt(acc if i != on_v[-1] else res, acc, x, A.add)
        tt(res, sums, res, A.add)
        out(T.yz, 4, 3072, 2, "act")

    do("load", load)
    scores(0), extend(0), elect(0), column(0)
    scores(2), elect(2)
    scores(1), extend(1), elect(1), column(1)
    extend(2), column(2)
    do("exp0", exp_c, 0), do("exp2", exp_c, 2), do("fold0", fold, 0), out(T.ym, 0, 0)
    sizes(0, (3, 4))
    scores(3), extend(3), elect(3), column(3)
    do("exp1", exp_c, 1), do("exp3", exp_c, 3), do("fold1", fold, 1), out(T.ym, 1, 512), out(T.ym, 3, 768)
    sizes(1, (4,)), by_maxima(0, 1)
    do("read01", exp_r, 0, 1, [i for i in range(16) if i not in (3, 4)]), do("fold2", fold, 2)
    scores(5), scores(4), extend(4), elect(5), elect(4), column(4), extend(5), column(5)
    sizes(2), sizes(3), by_maxima(2, 3)
    do("again", again), out(T.yz, 0, 1024, 2)
    do("exp5", exp_c, 5), do("exp4", exp_c, 4), do("fold3", fold, 3), do("fold4", fold, 4), out(T.ym, 4, 1792)
    do("upper2", upper, 2, 0, 512, 256), do("upper5", upper, 5, 768, 1792, 1536)
    do("read23", exp_r, 2, 3, range(16)), do("fold5", fold, 5), do("fold6", fold, 6)
    sizes(4), sizes(5), by_maxima(4, 5)
    do("tail", tail)
    do("join", tt, v("R", 0, 512), v("R", 0, 512), v("R", 2048, 2560), A.add), out(T.yz, 2, 0, 2)

    if not PLAN:
        deps = overlap_deps(ops, range(len(ops)), regs, False)
        for k, o in enumerate(ops):
            deps[k] |= set(o["follows"])
        PLAN["ops"], PLAN["d0"] = ops, deps
        PLAN["order"], PLAN["ring"], PLAN["took"] = plan(ops, deps)
    ring.update(PLAN["ring"])
    for k, o in enumerate(ops):
        if PLAN["took"][k] != o["q"]:
            o["q"], o["fn"], o["was"] = "act", [o["alt"]], "dve"
    if "deps" not in PLAN:
        PLAN["deps"] = overlap_deps(ops, PLAN["order"], regs, True)
    order, deps = PLAN["order"], PLAN["deps"]

    needed = set()
    for k in order:
        if ops[k]["q"] != "far":
            needed |= deps[k]
    count = {}
    for k in order:
        o = ops[k]
        if o["sem"] is not None:
            o["done"] = (o["sem"], abs(o["inc"]))
        elif k in needed:
            count[o["q"]] = count.get(o["q"], 0) + 1
            o["done"] = (o["q"], count[o["q"]])
    queue = {"pe": g.tensor, "act": g.scalar, "dve": g.vector, "pool": g, "sp": g.sync}
    known = {q: {} for q in queue}
    place = {k: j for j, k in enumerate(order)}
    for k in order:
        o = ops[k]
        if o["q"] == "far":
            o["clock"] = {}
            continue
        kn = known[o["q"]]
        for d in sorted(deps[k], key=lambda d: -place[d]):
            s, n = ops[d]["done"]
            if kn.get(s, 0) < n:
                queue[o["q"]].wait_ge(T.sem[s], n)
                kn[s] = n
                for s2, n2 in ops[d]["clock"].items():
                    kn[s2] = max(kn.get(s2, 0), n2)
        o["clock"] = dict(kn)
        for fn in o["fn"]:
            ins = fn()
        if "done" in o and o["inc"] > 0:
            ins.then_inc(T.sem[o["done"][0]], o["inc"])
    for o in ops:
        if o["sem"] is not None and max(kn.get(o["sem"], 0) for kn in known.values()) < abs(o["inc"]):
            g.wait_ge(T.sem[o["sem"]], abs(o["inc"]))
